import numpy as np
import ml_dtypes


def mxq(x, axis, fmt="e4m3"):
    dtype, down = {"e4m3": (ml_dtypes.float8_e4m3fn, 7), "e5m2": (ml_dtypes.float8_e5m2, 14)}[fmt]
    v = np.moveaxis(np.asarray(x, np.float32).astype(ml_dtypes.bfloat16).astype(np.float64), axis, -1)
    blocks = v.reshape(v.shape[:-1] + (-1, 32))
    amax = np.abs(blocks).max(-1, keepdims=True)
    byte = np.maximum(np.where(amax > 0, np.frexp(amax)[1] - 1 + 127, 0) - down, 1)
    scale = np.exp2(byte - 127.0)
    codes = (blocks / scale).astype(np.float32).astype(dtype).astype(np.float64)
    return np.moveaxis((codes * scale).reshape(v.shape), -1, axis)


WIDE = False


def mx_kscale(k):
    if not WIDE:
        return np.ones(k)
    levels = np.array([10, -10, 5, -5, 0])
    if k % 512:
        return np.exp2(np.random.permutation(np.resize(levels, k // 32))).repeat(32)
    a = np.empty((k // 512, 16))
    for p in range(k // 512):
        a[p, :8] = np.random.permutation(np.resize(levels, 8))
        for g in range(8):
            far = levels[np.abs(levels - a[p, g]) >= 10]
            a[p, g + 8] = far[np.random.randint(len(far))]
    return np.exp2(a.ravel()).repeat(32)


def f64(x):
    return np.asarray(x).astype(np.float64)


def striped(idx):
    return np.tile(idx.reshape(-1, 16).T, (8, 1)).astype(np.uint16)


def unstriped(offs):
    return offs[:16].T.reshape(-1).astype(np.int64)


def pack_weight(w):
    k, n = w.shape
    w = f64(np.asarray(w, np.float32).astype(ml_dtypes.bfloat16)).reshape(k // 32, 32, n)
    amax = np.abs(w).max(1)
    byte = np.clip(np.where(amax > 0, np.frexp(amax)[1] - 1 + 127 - 7, 1), 1, 254)
    scaled = (w * np.exp2(127.0 - byte)[:, None, :]).reshape(k, n).astype(np.float32)
    words = np.ascontiguousarray(scaled.reshape(k // 512, 128, 4, n).transpose(0, 1, 3, 2)).astype(ml_dtypes.float8_e4m3fn).view(np.uint8)
    return words, np.ascontiguousarray(byte.astype(np.uint8).reshape(k // 512, 16, n))


def unpack_weight(words, scales):
    g, p, n, _ = words.shape
    vals = np.ascontiguousarray(words).view(ml_dtypes.float8_e4m3fn).astype(np.float64) * np.repeat(np.exp2(scales.astype(np.float64) - 127.0), 8, axis=1)[..., None]
    return vals.transpose(0, 1, 3, 2).reshape(g * 512, n)


def gelu(v):
    return 0.5 * v * (1.0 + np.tanh(np.sqrt(2.0 / np.pi) * (v + 0.044715 * v**3)))


K, T, S, H, N = 1024, 1024, 512, 512, 128


def setup_inputs():
    n = np.random.standard_normal
    s = mx_kscale(K)[:, None]
    u = mx_kscale(H)
    packed_w1 = pack_weight(n((K, N)) / np.sqrt(2 * K) / s)
    packed_w3 = pack_weight(n((H, N)) / np.sqrt(2 * H) / u[:, None])
    return {
        "xT": (n((K, T)) * s).astype(np.float32),
        "w1_words": packed_w1[0],
        "w1_scales": packed_w1[1],
        "w2": (n((K, H)) / np.sqrt(K) / s * u).astype(np.float32),
        "w3_words": packed_w3[0],
        "w3_scales": packed_w3[1],
        "offs": striped(np.random.permutation(T)[:S]),
    }


def reference(xT, w1_words, w1_scales, w2, w3_words, w3_scales, offs):
    xq = mxq(f64(xT)[:, unstriped(offs)], 0, "e4m3")
    h = gelu(mxq(f64(w2), 0, "e4m3").T @ xq)
    return unpack_weight(w1_words, w1_scales).T @ xq + unpack_weight(w3_words, w3_scales).T @ mxq(h, 0, "e4m3")

@@ -1,0 +1,153 @@
+from contextlib import ExitStack
+
+import concourse.mybir as mybir
+
+K, T, S, H, N = 1024, 1024, 512, 512, 128
+FLOPS = 2 * S * (K * H + K * N + H * N)
+
+F32 = mybir.dt.float32
+BF16 = mybir.dt.bfloat16
+U32 = mybir.dt.uint32
+I32 = mybir.dt.int32
+U16 = mybir.dt.uint16
+U8 = mybir.dt.uint8
+FP8X4 = mybir.dt.float8_e4m3fn_x4
+GELU = mybir.ActivationFunctionType.Gelu_apprx_tanh
+
+P = 128
+PACK = 4
+K_PASS = P * PACK
+PASSES = K // K_PASS
+CHUNK = 128
+CHUNKS = S // CHUNK
+HALF = H // 2
+M_HALF = HALF // PACK
+
+X_PIECES = ((0, 0, 512, 192), (0, 512, 512, 128), (1, 0, 512, 128), (1, 512, 256, 96), (1, 768, 256, 160))
+W_PIECES = ((0, 0, 0), (0, 1, 16), (1, 0, 24), (1, 1, 40))
+
+
+def tile_picked_lora_gelu_e_kernel(
+    tc, xT, w1_words, w1_scales, w2, w3_words, w3_scales, offs, out
+):
+    nc = tc.nc
+    with ExitStack() as ctx:
+        keep = ctx.enter_context(tc.tile_pool(name="keep", bufs=1))
+        psum = ctx.enter_context(tc.psum_pool(name="psum", bufs=1))
+
+        def sb(name, shape, dtype):
+            return keep.tile(shape, dtype, name=name, align_bytes=64)
+
+        offsets = keep.tile([P, S // 16], U16, name="offsets")
+        nc.sync.dma_start(offsets[:], offs)
+
+        warm = sb("warm", [P, 8], F32)
+        warm_out = sb("warm_out", [P, 8], F32)
+        nc.vector.memset(warm[:], 0.0)
+        nc.scalar.activation(warm_out[:], warm[:], GELU)
+
+        all_bytes = sb("all_bytes", [P, T], U8)
+        w1_s = sb("w1_s", [P, PASSES, N], U8)
+        w3_s = sb("w3_s", [P, N], U8)
+        nc.vector.memset(w1_s[:].bitcast(I32), 0)
+        nc.vector.memset(w3_s[:].bitcast(I32), 0)
+        nc.vector.memset(all_bytes[:].bitcast(I32), 0)
+
+        x_raw = []
+        for i, (z, t0, n, nv) in enumerate(X_PIECES):
+            raw = sb("x_raw%d" % i, [P, PACK, n], F32)
+            rows = xT[z * K_PASS : (z + 1) * K_PASS, t0 : t0 + n]
+            nc.sync.dma_start(raw[:], rows.rearrange("(p j) c -> p j c", j=PACK))
+            x_raw.append(raw)
+        w1_w = sb("w1_w", [P, PASSES, N], U32)
+        nc.sync.dma_start(w1_w[:].bitcast(I32), w1_words.rearrange("z p c r -> p z (c r)").bitcast(I32))
+        w1_rows = w1_scales.rearrange("z (q r) c -> r q z c", r=4)
+        for r in range(4):
+            nc.sync.dma_start(w1_s[r:P:32, :, :].bitcast(I32), w1_rows[r].bitcast(I32))
+        w_raw = []
+        for i, (z, half, mv) in enumerate(W_PIECES):
+            raw = sb("w_raw%d" % i, [P, PACK, HALF], F32)
+            rows = w2[z * K_PASS : (z + 1) * K_PASS, half * HALF : (half + 1) * HALF]
+            nc.sync.dma_start(raw[:], rows.rearrange("(p j) c -> p j c", j=PACK))
+            w_raw.append(raw)
+        w3_w = sb("w3_w", [P, N], U32)
+        nc.sync.dma_start(w3_w[:].bitcast(I32), w3_words[0].rearrange("p c r -> p (c r)").bitcast(I32))
+        w3_rows = w3_scales[0].rearrange("(q r) c -> r q c", r=4)
+        for r in range(4):
+            nc.sync.dma_start(w3_s[r:P:32, :].bitcast(I32), w3_rows[r].bitcast(I32))
+
+        all_words = [sb("all_words%d" % z, [P, T], U32) for z in range(PASSES)]
+        x_words = [sb("x_words%d" % z, [P, S], U32) for z in range(PASSES)]
+        x_bytes = sb("x_bytes", [P, S], U8)
+        for i, (z, t0, n, nv) in enumerate(X_PIECES):
+            grouped = sb("x_bf%d" % i, [P, n * PACK], BF16)
+            dst = grouped[:].rearrange("p (c i j) -> p c j i", i=4, j=PACK)
+            src = x_raw[i][:].rearrange("p j (c i) -> p c j i", i=4)
+            nc.scalar.copy(dst[:, nv // 4 :], src[:, nv // 4 :])
+            nc.vector.tensor_copy(dst[:, : nv // 4], src[:, : nv // 4])
+            nc.vector.quantize_mx(
+                all_words[z][:, t0 : t0 + n].bitcast(FP8X4), all_bytes[4 * z : P, t0 : t0 + n], grouped[:]
+            )
+            if t0 + n == T:
+                nc.vector.tensor_copy(x_words[z][:], all_words[z][:].indirect(offsets[:]))
+        nc.vector.tensor_copy(x_bytes[:], all_bytes[:].indirect(offsets[:]))
+
+        def x_operand(z, c):
+            cols = slice(c * CHUNK, (c + 1) * CHUNK)
+            return dict(rhs=x_words[z][:, cols].bitcast(FP8X4), rhs_scale=x_bytes[4 * z : P, cols])
+
+        out_banks = [psum.tile([P, CHUNK], F32, name="out_bank%d" % c) for c in range(CHUNKS)]
+        h_banks = [psum.tile([P, PACK, CHUNK], F32, name="h_bank%d" % c) for c in range(CHUNKS)]
+        for z in range(PASSES):
+            for c in range(CHUNKS):
+                nc.tensor.matmul_mx(
+                    out_banks[c][:], lhsT=w1_w[:, z, :].bitcast(FP8X4), lhsT_scale=w1_s[:, z, :],
+                    start=(z == 0), stop=False, **x_operand(z, c)
+                )
+
+        w2_words = [sb("w2_words%d" % z, [P, H], U32) for z in range(PASSES)]
+        w2_bytes = [sb("w2_bytes%d" % z, [P, H], U8) for z in range(PASSES)]
+
+        def h_pass(z, c, t):
+            cols = slice(t * P, (t + 1) * P)
+            nc.tensor.matmul_mx(
+                h_banks[c][:, t, :], lhsT=w2_words[z][:, cols].bitcast(FP8X4), lhsT_scale=w2_bytes[z][:, cols],
+                start=(z == 0 and t == 0), stop=(z == PASSES - 1 and t == PACK - 1), **x_operand(z, c)
+            )
+
+        for i, (z, half, mv) in enumerate(W_PIECES):
+            grouped = sb("w_bf%d" % i, [P, PACK * M_HALF * PACK], BF16)
+            dst = grouped[:].rearrange("p (t m j) -> p m j t", t=PACK, j=PACK)
+            src = w_raw[i][:].rearrange("p j (m t) -> p m j t", t=PACK)
+            nc.scalar.copy(dst[:, mv:], src[:, mv:])
+            if mv:
+                nc.vector.tensor_copy(dst[:, :mv], src[:, :mv])
+            for t in range(PACK):
+                cols = slice(t * P + half * M_HALF, t * P + (half + 1) * M_HALF)
+                nc.vector.quantize_mx(
+                    w2_words[z][:, cols].bitcast(FP8X4), w2_bytes[z][:, cols],
+                    grouped[:, t * M_HALF * PACK : (t + 1) * M_HALF * PACK],
+                )
+            if z == 0 and half == 1:
+                for t in range(PACK):
+                    for c in range(CHUNKS):
+                        h_pass(0, c, t)
+
+        for c in range(CHUNKS):
+            for t in range(PACK):
+                h_pass(1, c, t)
+        for c in range(CHUNKS):
+            h_bf = sb("h_bf%d" % c, [P, CHUNK * PACK], BF16)
+            nc.scalar.activation(
+                h_bf[:].rearrange("p (n t) -> p n t", t=PACK), h_banks[c][:].rearrange("p t n -> p n t"), GELU
+            )
+            h_words = sb("h_words%d" % c, [P, CHUNK], U32)
+            h_bytes = sb("h_bytes%d" % c, [P, CHUNK], U8)
+            nc.vector.quantize_mx(h_words[:].bitcast(FP8X4), h_bytes[:], h_bf[:])
+            nc.tensor.matmul_mx(
+                out_banks[c][:], lhsT=w3_w[:].bitcast(FP8X4), lhsT_scale=w3_s[:],
+                rhs=h_words[:].bitcast(FP8X4), rhs_scale=h_bytes[:], start=False, stop=True,
+            )
+            result = sb("result%d" % c, [P, CHUNK], F32)
+            nc.vector.tensor_copy(result[:], out_banks[c][:])
+            nc.sync.dma_start(out[:, c * CHUNK : (c + 1) * CHUNK], result[:])

@@ -20,11 +20,10 @@ K_PASS = P * PACK
 PASSES = K // K_PASS
 CHUNK = 128
 CHUNKS = S // CHUNK
-HALF = H // 2
-M_HALF = HALF // PACK
 
-X_PIECES = ((0, 0, 512, 192), (0, 512, 512, 128), (1, 0, 512, 128), (1, 512, 256, 96), (1, 768, 256, 160))
-W_PIECES = ((0, 0, 0), (0, 1, 16), (1, 0, 24), (1, 1, 40))
+X_PIECES = ((0, 0, 1024, 512), (1, 0, 512, 0), (1, 512, 512, 256))
+S_STEP = 256
+W0_VECTOR = 32
 
 
 def tile_picked_lora_gelu_e_kernel(
@@ -38,9 +37,6 @@ def tile_picked_lora_gelu_e_kernel(
         def sb(name, shape, dtype):
             return keep.tile(shape, dtype, name=name, align_bytes=64)
 
-        offsets = keep.tile([P, S // 16], U16, name="offsets")
-        nc.sync.dma_start(offsets[:], offs)
-
         warm = sb("warm", [P, 8], F32)
         warm_out = sb("warm_out", [P, 8], F32)
         nc.vector.memset(warm[:], 0.0)
@@ -53,101 +49,119 @@ def tile_picked_lora_gelu_e_kernel(
         nc.vector.memset(w3_s[:].bitcast(I32), 0)
         nc.vector.memset(all_bytes[:].bitcast(I32), 0)
 
+        offsets = keep.tile([P, S // 16], U16, name="offsets")
         x_raw = []
         for i, (z, t0, n, nv) in enumerate(X_PIECES):
             raw = sb("x_raw%d" % i, [P, PACK, n], F32)
             rows = xT[z * K_PASS : (z + 1) * K_PASS, t0 : t0 + n]
             nc.sync.dma_start(raw[:], rows.rearrange("(p j) c -> p j c", j=PACK))
             x_raw.append(raw)
-        w1_w = sb("w1_w", [P, PASSES, N], U32)
-        nc.sync.dma_start(w1_w[:].bitcast(I32), w1_words.rearrange("z p c r -> p z (c r)").bitcast(I32))
-        w1_rows = w1_scales.rearrange("z (q r) c -> r q z c", r=4)
-        for r in range(4):
-            nc.sync.dma_start(w1_s[r:P:32, :, :].bitcast(I32), w1_rows[r].bitcast(I32))
+            if i == 0:
+                nc.sync.dma_start(offsets[:], offs)
         w_raw = []
-        for i, (z, half, mv) in enumerate(W_PIECES):
-            raw = sb("w_raw%d" % i, [P, PACK, HALF], F32)
-            rows = w2[z * K_PASS : (z + 1) * K_PASS, half * HALF : (half + 1) * HALF]
+        for z in range(PASSES):
+            raw = sb("w_raw%d" % z, [P, PACK, H], F32)
+            rows = w2[z * K_PASS : (z + 1) * K_PASS, :]
             nc.sync.dma_start(raw[:], rows.rearrange("(p j) c -> p j c", j=PACK))
             w_raw.append(raw)
+        w1_w = sb("w1_w", [P, PASSES, N], U32)
+        nc.sync.dma_start(w1_w[:].bitcast(I32), w1_words.rearrange("z p c r -> p z (c r)").bitcast(I32))
         w3_w = sb("w3_w", [P, N], U32)
         nc.sync.dma_start(w3_w[:].bitcast(I32), w3_words[0].rearrange("p c r -> p (c r)").bitcast(I32))
+        w1_rows = w1_scales.rearrange("z (q r) c -> r q z c", r=4)
+        for r in range(4):
+            nc.gpsimd.dma_start(w1_s[r:P:32, :, :].bitcast(I32), w1_rows[r].bitcast(I32))
         w3_rows = w3_scales[0].rearrange("(q r) c -> r q c", r=4)
         for r in range(4):
-            nc.sync.dma_start(w3_s[r:P:32, :].bitcast(I32), w3_rows[r].bitcast(I32))
+            nc.gpsimd.dma_start(w3_s[r:P:32, :].bitcast(I32), w3_rows[r].bitcast(I32))
 
         all_words = [sb("all_words%d" % z, [P, T], U32) for z in range(PASSES)]
-        x_words = [sb("x_words%d" % z, [P, S], U32) for z in range(PASSES)]
+        x_words0 = sb("x_words0", [P, S], U32)
+        x_words1 = [sb("x_words1a", [P, S // 2], U32)]
         x_bytes = sb("x_bytes", [P, S], U8)
         for i, (z, t0, n, nv) in enumerate(X_PIECES):
             grouped = sb("x_bf%d" % i, [P, n * PACK], BF16)
             dst = grouped[:].rearrange("p (c i j) -> p c j i", i=4, j=PACK)
             src = x_raw[i][:].rearrange("p j (c i) -> p c j i", i=4)
-            nc.scalar.copy(dst[:, nv // 4 :], src[:, nv // 4 :])
-            nc.vector.tensor_copy(dst[:, : nv // 4], src[:, : nv // 4])
-            nc.vector.quantize_mx(
-                all_words[z][:, t0 : t0 + n].bitcast(FP8X4), all_bytes[4 * z : P, t0 : t0 + n], grouped[:]
-            )
-            if t0 + n == T:
-                nc.vector.tensor_copy(x_words[z][:], all_words[z][:].indirect(offsets[:]))
+            parts = [(0, nv)]
+            while parts[-1][1] < n:
+                parts.append((parts[-1][1], min(n, (parts[-1][1] // S_STEP + 1) * S_STEP)))
+            for a, b in parts[1:]:
+                nc.scalar.copy(dst[:, a // 4 : b // 4], src[:, a // 4 : b // 4])
+            if nv:
+                nc.vector.tensor_copy(dst[:, : nv // 4], src[:, : nv // 4])
+            for a, b in parts[0 if nv else 1 :]:
+                cols = slice(t0 + a, t0 + b)
+                nc.vector.quantize_mx(
+                    all_words[z][:, cols].bitcast(FP8X4), all_bytes[4 * z : P, cols],
+                    grouped[:, a * PACK : b * PACK],
+                )
+            if z == 0:
+                nc.vector.tensor_copy(x_words0[:], all_words[0][:].indirect(offsets[:]))
         nc.vector.tensor_copy(x_bytes[:], all_bytes[:].indirect(offsets[:]))
+        nc.vector.tensor_copy(x_words1[0][:], all_words[1][:].indirect(offsets[:, : S // 32]))
 
         def x_operand(z, c):
             cols = slice(c * CHUNK, (c + 1) * CHUNK)
-            return dict(rhs=x_words[z][:, cols].bitcast(FP8X4), rhs_scale=x_bytes[4 * z : P, cols])
-
-        out_banks = [psum.tile([P, CHUNK], F32, name="out_bank%d" % c) for c in range(CHUNKS)]
-        h_banks = [psum.tile([P, PACK, CHUNK], F32, name="h_bank%d" % c) for c in range(CHUNKS)]
-        for z in range(PASSES):
-            for c in range(CHUNKS):
-                nc.tensor.matmul_mx(
-                    out_banks[c][:], lhsT=w1_w[:, z, :].bitcast(FP8X4), lhsT_scale=w1_s[:, z, :],
-                    start=(z == 0), stop=False, **x_operand(z, c)
-                )
+            words = x_words0[:, cols] if z == 0 else x_words1[c // 2][:, (c % 2) * CHUNK : (c % 2 + 1) * CHUNK]
+            return dict(rhs=words.bitcast(FP8X4), rhs_scale=x_bytes[4 * z : P, cols])
 
         w2_words = [sb("w2_words%d" % z, [P, H], U32) for z in range(PASSES)]
         w2_bytes = [sb("w2_bytes%d" % z, [P, H], U8) for z in range(PASSES)]
-
-        def h_pass(z, c, t):
-            cols = slice(t * P, (t + 1) * P)
-            nc.tensor.matmul_mx(
-                h_banks[c][:, t, :], lhsT=w2_words[z][:, cols].bitcast(FP8X4), lhsT_scale=w2_bytes[z][:, cols],
-                start=(z == 0 and t == 0), stop=(z == PASSES - 1 and t == PACK - 1), **x_operand(z, c)
+        grouped = sb("w_bf0", [P, H * PACK], BF16)
+        dst = grouped[:].rearrange("p (t m j) -> p m j t", t=PACK, j=PACK)
+        src = w_raw[0][:].rearrange("p j (m t) -> p m j t", t=PACK)
+        nc.scalar.copy(dst[:, W0_VECTOR:], src[:, W0_VECTOR:])
+        nc.vector.tensor_copy(dst[:, :W0_VECTOR], src[:, :W0_VECTOR])
+        for u in range(2):
+            cols = slice(u * 2 * P, (u + 1) * 2 * P)
+            nc.vector.quantize_mx(
+                w2_words[0][:, cols].bitcast(FP8X4), w2_bytes[0][:, cols],
+                grouped[:, u * 2 * P * PACK : (u + 1) * 2 * P * PACK],
             )
+        src = w_raw[1][:].rearrange("p j (m t) -> p m j t", t=PACK)
+        halves = [keep.tile([P, 2 * P * PACK], BF16, name="w_bf1_%d" % u, tag="w_bf1_%d" % u, align_bytes=64) for u in range(2)]
+        nc.scalar.copy(halves[1][:].rearrange("p (t m j) -> p m j t", t=2, j=PACK), src[:, :, :, 2:4])
+        nc.vector.tensor_copy(halves[0][:].rearrange("p (t m j) -> p m j t", t=2, j=PACK), src[:, :, :, 0:2])
+        for u in range(2):
+            cols = slice(u * 2 * P, (u + 1) * 2 * P)
+            nc.vector.quantize_mx(w2_words[1][:, cols].bitcast(FP8X4), w2_bytes[1][:, cols], halves[u][:])
+        x_words1.append(keep.tile([P, S // 2], U32, name="x_words1b", tag="w_bf1_1", align_bytes=64))
+        nc.vector.tensor_copy(x_words1[1][:], all_words[1][:].indirect(offsets[:, S // 32 :]))
 
-        for i, (z, half, mv) in enumerate(W_PIECES):
-            grouped = sb("w_bf%d" % i, [P, PACK * M_HALF * PACK], BF16)
-            dst = grouped[:].rearrange("p (t m j) -> p m j t", t=PACK, j=PACK)
-            src = w_raw[i][:].rearrange("p j (m t) -> p m j t", t=PACK)
-            nc.scalar.copy(dst[:, mv:], src[:, mv:])
-            if mv:
-                nc.vector.tensor_copy(dst[:, :mv], src[:, :mv])
-            for t in range(PACK):
-                cols = slice(t * P + half * M_HALF, t * P + (half + 1) * M_HALF)
-                nc.vector.quantize_mx(
-                    w2_words[z][:, cols].bitcast(FP8X4), w2_bytes[z][:, cols],
-                    grouped[:, t * M_HALF * PACK : (t + 1) * M_HALF * PACK],
+        h_banks = [psum.tile([P, PACK, CHUNK], F32, name="h_bank%d" % c, tag="bank%d" % c) for c in range(CHUNKS)]
+
+        def h_pass(z, c, ts):
+            for t in ts:
+                cols = slice(t * P, (t + 1) * P)
+                nc.tensor.matmul_mx(
+                    h_banks[c][:, t, :], lhsT=w2_words[z][:, cols].bitcast(FP8X4), lhsT_scale=w2_bytes[z][:, cols],
+                    start=(z == 0 and t == 0), stop=(z == PASSES - 1 and t == PACK - 1), **x_operand(z, c)
                 )
-            if z == 0 and half == 1:
-                for t in range(PACK):
-                    for c in range(CHUNKS):
-                        h_pass(0, c, t)
 
+        for u in range(2):
+            for c in range(CHUNKS):
+                h_pass(0, c, (2 * u, 2 * u + 1))
         for c in range(CHUNKS):
-            for t in range(PACK):
-                h_pass(1, c, t)
+            h_pass(1, c, range(PACK))
         for c in range(CHUNKS):
             h_bf = sb("h_bf%d" % c, [P, CHUNK * PACK], BF16)
             nc.scalar.activation(
                 h_bf[:].rearrange("p (n t) -> p n t", t=PACK), h_banks[c][:].rearrange("p t n -> p n t"), GELU
             )
+            out_bank = psum.tile([P, CHUNK], F32, name="out_bank%d" % c, tag="bank%d" % c)
+            for z in range(PASSES):
+                nc.tensor.matmul_mx(
+                    out_bank[:], lhsT=w1_w[:, z, :].bitcast(FP8X4), lhsT_scale=w1_s[:, z, :],
+                    start=(z == 0), stop=False, **x_operand(z, c)
+                )
             h_words = sb("h_words%d" % c, [P, CHUNK], U32)
             h_bytes = sb("h_bytes%d" % c, [P, CHUNK], U8)
             nc.vector.quantize_mx(h_words[:].bitcast(FP8X4), h_bytes[:], h_bf[:])
             nc.tensor.matmul_mx(
-                out_banks[c][:], lhsT=w3_w[:].bitcast(FP8X4), lhsT_scale=w3_s[:],
+                out_bank[:], lhsT=w3_w[:].bitcast(FP8X4), lhsT_scale=w3_s[:],
                 rhs=h_words[:].bitcast(FP8X4), rhs_scale=h_bytes[:], start=False, stop=True,
             )
             result = sb("result%d" % c, [P, CHUNK], F32)
-            nc.vector.tensor_copy(result[:], out_banks[c][:])
+            nc.vector.tensor_copy(result[:], out_bank[:])
             nc.sync.dma_start(out[:, c * CHUNK : (c + 1) * CHUNK], result[:])

@@ -21,9 +21,10 @@ PASSES = K // K_PASS
 CHUNK = 128
 CHUNKS = S // CHUNK
 
-X_PIECES = ((0, 0, 1024, 512), (1, 0, 512, 0), (1, 512, 512, 256))
-S_STEP = 256
-W0_VECTOR = 32
+X_PIECES = ((0, 0, 512, 256), (0, 512, 512, 256), (1, 0, 512, 128), (1, 512, 256, 128), (1, 768, 256, 128))
+W_PIECES = ((0, 0, 0), (0, 1, 16), (1, 0, 0), (1, 1, 40))
+HALF = H // 2
+M_HALF = HALF // PACK
 
 
 def tile_picked_lora_gelu_e_kernel(
@@ -32,6 +33,7 @@ def tile_picked_lora_gelu_e_kernel(
     nc = tc.nc
     with ExitStack() as ctx:
         keep = ctx.enter_context(tc.tile_pool(name="keep", bufs=1))
+        late = ctx.enter_context(tc.tile_pool(name="late", bufs=1))
         psum = ctx.enter_context(tc.psum_pool(name="psum", bufs=1))
 
         def sb(name, shape, dtype):
@@ -59,9 +61,9 @@ def tile_picked_lora_gelu_e_kernel(
             if i == 0:
                 nc.sync.dma_start(offsets[:], offs)
         w_raw = []
-        for z in range(PASSES):
-            raw = sb("w_raw%d" % z, [P, PACK, H], F32)
-            rows = w2[z * K_PASS : (z + 1) * K_PASS, :]
+        for i, (z, half, mv) in enumerate(W_PIECES):
+            raw = sb("w_raw%d" % i, [P, PACK, HALF], F32)
+            rows = w2[z * K_PASS : (z + 1) * K_PASS, half * HALF : (half + 1) * HALF]
             nc.sync.dma_start(raw[:], rows.rearrange("(p j) c -> p j c", j=PACK))
             w_raw.append(raw)
         w1_w = sb("w1_w", [P, PASSES, N], U32)
@@ -78,56 +80,53 @@ def tile_picked_lora_gelu_e_kernel(
         all_words = [sb("all_words%d" % z, [P, T], U32) for z in range(PASSES)]
         x_words0 = sb("x_words0", [P, S], U32)
         x_words1 = [sb("x_words1a", [P, S // 2], U32)]
-        x_bytes = sb("x_bytes", [P, S], U8)
+        x_bytes = [sb("x_bytes_a", [P, S - CHUNK], U8)]
         for i, (z, t0, n, nv) in enumerate(X_PIECES):
             grouped = sb("x_bf%d" % i, [P, n * PACK], BF16)
             dst = grouped[:].rearrange("p (c i j) -> p c j i", i=4, j=PACK)
             src = x_raw[i][:].rearrange("p j (c i) -> p c j i", i=4)
-            parts = [(0, nv)]
-            while parts[-1][1] < n:
-                parts.append((parts[-1][1], min(n, (parts[-1][1] // S_STEP + 1) * S_STEP)))
-            for a, b in parts[1:]:
-                nc.scalar.copy(dst[:, a // 4 : b // 4], src[:, a // 4 : b // 4])
+            nc.scalar.copy(dst[:, nv // 4 :], src[:, nv // 4 :])
             if nv:
                 nc.vector.tensor_copy(dst[:, : nv // 4], src[:, : nv // 4])
-            for a, b in parts[0 if nv else 1 :]:
+            for a, b in ((0, nv), (nv, n)) if z == 0 else ((0, n),):
                 cols = slice(t0 + a, t0 + b)
                 nc.vector.quantize_mx(
-                    all_words[z][:, cols].bitcast(FP8X4), all_bytes[4 * z : P, cols],
-                    grouped[:, a * PACK : b * PACK],
+                    all_words[z][:, cols].bitcast(FP8X4), all_bytes[4 * z : P, cols], grouped[:, a * PACK : b * PACK]
                 )
-            if z == 0:
+            if z == 0 and t0 + n == T:
                 nc.vector.tensor_copy(x_words0[:], all_words[0][:].indirect(offsets[:]))
-        nc.vector.tensor_copy(x_bytes[:], all_bytes[:].indirect(offsets[:]))
+        nc.vector.tensor_copy(x_bytes[0][:], all_bytes[:].indirect(offsets[:, : (S - CHUNK) // 16]))
         nc.vector.tensor_copy(x_words1[0][:], all_words[1][:].indirect(offsets[:, : S // 32]))
 
         def x_operand(z, c):
             cols = slice(c * CHUNK, (c + 1) * CHUNK)
             words = x_words0[:, cols] if z == 0 else x_words1[c // 2][:, (c % 2) * CHUNK : (c % 2 + 1) * CHUNK]
-            return dict(rhs=words.bitcast(FP8X4), rhs_scale=x_bytes[4 * z : P, cols])
+            return dict(rhs=words.bitcast(FP8X4), rhs_scale=x_bytes[0][4 * z : P, cols] if c < CHUNKS - 1 else x_bytes[1][4 * z : P, :])
 
         w2_words = [sb("w2_words%d" % z, [P, H], U32) for z in range(PASSES)]
         w2_bytes = [sb("w2_bytes%d" % z, [P, H], U8) for z in range(PASSES)]
-        grouped = sb("w_bf0", [P, H * PACK], BF16)
-        dst = grouped[:].rearrange("p (t m j) -> p m j t", t=PACK, j=PACK)
-        src = w_raw[0][:].rearrange("p j (m t) -> p m j t", t=PACK)
-        nc.scalar.copy(dst[:, W0_VECTOR:], src[:, W0_VECTOR:])
-        nc.vector.tensor_copy(dst[:, :W0_VECTOR], src[:, :W0_VECTOR])
-        for u in range(2):
-            cols = slice(u * 2 * P, (u + 1) * 2 * P)
-            nc.vector.quantize_mx(
-                w2_words[0][:, cols].bitcast(FP8X4), w2_bytes[0][:, cols],
-                grouped[:, u * 2 * P * PACK : (u + 1) * 2 * P * PACK],
-            )
-        src = w_raw[1][:].rearrange("p j (m t) -> p m j t", t=PACK)
-        halves = [keep.tile([P, 2 * P * PACK], BF16, name="w_bf1_%d" % u, tag="w_bf1_%d" % u, align_bytes=64) for u in range(2)]
-        nc.scalar.copy(halves[1][:].rearrange("p (t m j) -> p m j t", t=2, j=PACK), src[:, :, :, 2:4])
-        nc.vector.tensor_copy(halves[0][:].rearrange("p (t m j) -> p m j t", t=2, j=PACK), src[:, :, :, 0:2])
-        for u in range(2):
-            cols = slice(u * 2 * P, (u + 1) * 2 * P)
-            nc.vector.quantize_mx(w2_words[1][:, cols].bitcast(FP8X4), w2_bytes[1][:, cols], halves[u][:])
-        x_words1.append(keep.tile([P, S // 2], U32, name="x_words1b", tag="w_bf1_1", align_bytes=64))
+        w_bf = [
+            sb("w_bf0", [P, H * PACK], BF16),
+            late.tile([P, H * PACK], BF16, name="w_bf1", offset=0, align_bytes=64),
+        ]
+        for i, (z, half, mv) in enumerate(W_PIECES):
+            dst = w_bf[z][:].rearrange("p (t m j) -> p m j t", t=PACK, j=PACK)[:, half * M_HALF : (half + 1) * M_HALF]
+            src = w_raw[i][:].rearrange("p j (m t) -> p m j t", t=PACK)
+            nc.scalar.copy(dst[:, mv:], src[:, mv:])
+            if mv:
+                nc.vector.tensor_copy(dst[:, :mv], src[:, :mv])
+            if half == 1:
+                for u in range(2):
+                    cols = slice(u * 2 * P, (u + 1) * 2 * P)
+                    nc.vector.quantize_mx(
+                        w2_words[z][:, cols].bitcast(FP8X4), w2_bytes[z][:, cols],
+                        w_bf[z][:, u * 2 * P * PACK : (u + 1) * 2 * P * PACK],
+                    )
+
+        x_words1.append(late.tile([P, S // 2], U32, name="x_words1b", offset=0, align_bytes=64))
         nc.vector.tensor_copy(x_words1[1][:], all_words[1][:].indirect(offsets[:, S // 32 :]))
+        x_bytes.append(late.tile([P, CHUNK], U8, name="x_bytes_b", offset=1024, align_bytes=64))
+        nc.vector.tensor_copy(x_bytes[1][:], all_bytes[:].indirect(offsets[:, (S - CHUNK) // 16 :]))
 
         h_banks = [psum.tile([P, PACK, CHUNK], F32, name="h_bank%d" % c, tag="bank%d" % c) for c in range(CHUNKS)]
 
@@ -140,9 +139,11 @@ def tile_picked_lora_gelu_e_kernel(
                 )
 
         for u in range(2):
-            for c in range(CHUNKS):
+            for c in range(CHUNKS - 1):
                 h_pass(0, c, (2 * u, 2 * u + 1))
         for c in range(CHUNKS):
+            if c == CHUNKS - 1:
+                h_pass(0, c, range(PACK))
             h_pass(1, c, range(PACK))
         for c in range(CHUNKS):
             h_bf = sb("h_bf%d" % c, [P, CHUNK * PACK], BF16)

@@ -20,9 +20,10 @@ K_PASS = P * PACK
 PASSES = K // K_PASS
 CHUNK = 128
 CHUNKS = S // CHUNK
+LIST_COLS = CHUNK // 16
 
-X_PIECES = ((0, 0, 512, 256), (0, 512, 512, 256), (1, 0, 512, 128), (1, 512, 256, 128), (1, 768, 256, 128))
-W_PIECES = ((0, 0, 0), (0, 1, 16), (1, 0, 0), (1, 1, 40))
+X_PIECES = ((0, 0, 512, 256), (0, 512, 512, 320), (1, 0, 256, 0), (1, 256, 256, 0), (1, 512, 256, 128), (1, 768, 256, 160))
+W_PIECES = ((0, 0, 0), (0, 1, 2), (1, 0, 0), (1, 1, 2))
 HALF = H // 2
 M_HALF = HALF // PACK
 
@@ -36,18 +37,20 @@ def tile_picked_lora_gelu_e_kernel(
         late = ctx.enter_context(tc.tile_pool(name="late", bufs=1))
         psum = ctx.enter_context(tc.psum_pool(name="psum", bufs=1))
 
-        def sb(name, shape, dtype):
-            return keep.tile(shape, dtype, name=name, align_bytes=64)
+        def sb(name, shape, dtype, offset=None):
+            if offset is None:
+                return keep.tile(shape, dtype, name=name, align_bytes=64)
+            return late.tile(shape, dtype, name=name, offset=offset, align_bytes=64)
 
-        warm = sb("warm", [P, 8], F32)
-        warm_out = sb("warm_out", [P, 8], F32)
-        nc.vector.memset(warm[:], 0.0)
-        nc.scalar.activation(warm_out[:], warm[:], GELU)
+        zeros = sb("zeros", [P, 1], F32)
+        zero_bias = sb("zero_bias", [P, 1], F32)
+        nc.vector.memset(zeros[:], 0.0)
+        nc.scalar.activation(zero_bias[:], zeros[:], GELU)
 
         all_bytes = sb("all_bytes", [P, T], U8)
         w1_s = sb("w1_s", [P, PASSES, N], U8)
         w3_s = sb("w3_s", [P, N], U8)
-        nc.vector.memset(w1_s[:].bitcast(I32), 0)
+        nc.gpsimd.memset(w1_s[:].bitcast(I32), 0)
         nc.vector.memset(w3_s[:].bitcast(I32), 0)
         nc.vector.memset(all_bytes[:].bitcast(I32), 0)
 
@@ -62,71 +65,90 @@ def tile_picked_lora_gelu_e_kernel(
                 nc.sync.dma_start(offsets[:], offs)
         w_raw = []
         for i, (z, half, mv) in enumerate(W_PIECES):
-            raw = sb("w_raw%d" % i, [P, PACK, HALF], F32)
+            raw = sb("w_raw%d" % i, [P, PACK, HALF], F32, offset=8192 + 4096 * i)
             rows = w2[z * K_PASS : (z + 1) * K_PASS, half * HALF : (half + 1) * HALF]
             nc.sync.dma_start(raw[:], rows.rearrange("(p j) c -> p j c", j=PACK))
             w_raw.append(raw)
         w1_w = sb("w1_w", [P, PASSES, N], U32)
-        nc.sync.dma_start(w1_w[:].bitcast(I32), w1_words.rearrange("z p c r -> p z (c r)").bitcast(I32))
         w3_w = sb("w3_w", [P, N], U32)
-        nc.sync.dma_start(w3_w[:].bitcast(I32), w3_words[0].rearrange("p c r -> p (c r)").bitcast(I32))
+        nc.sync.dma_start(w1_w[:].bitcast(I32), w1_words.rearrange("z p c r -> p z (c r)").bitcast(I32))
         w1_rows = w1_scales.rearrange("z (q r) c -> r q z c", r=4)
         for r in range(4):
             nc.gpsimd.dma_start(w1_s[r:P:32, :, :].bitcast(I32), w1_rows[r].bitcast(I32))
+        nc.sync.dma_start(w3_w[:].bitcast(I32), w3_words[0].rearrange("p c r -> p (c r)").bitcast(I32))
         w3_rows = w3_scales[0].rearrange("(q r) c -> r q c", r=4)
         for r in range(4):
-            nc.gpsimd.dma_start(w3_s[r:P:32, :].bitcast(I32), w3_rows[r].bitcast(I32))
+            nc.sync.dma_start(w3_s[r:P:32, :].bitcast(I32), w3_rows[r].bitcast(I32))
 
         all_words = [sb("all_words%d" % z, [P, T], U32) for z in range(PASSES)]
-        x_words0 = sb("x_words0", [P, S], U32)
-        x_words1 = [sb("x_words1a", [P, S // 2], U32)]
-        x_bytes = [sb("x_bytes_a", [P, S - CHUNK], U8)]
+        x_words = [[None] * CHUNKS for z in range(PASSES)]
+        x_bytes = [None] * CHUNKS
+
+        def gather(kind, c0, c1, offset=None):
+            lists = offsets[:, c0 * LIST_COLS : c1 * LIST_COLS]
+            if kind == "bytes":
+                tile = sb("x_bytes%d" % c0, [P, (c1 - c0) * CHUNK], U8, offset)
+                nc.vector.tensor_copy(tile[:], all_bytes[:].indirect(lists))
+                views = x_bytes
+            else:
+                tile = sb("x_words%d_%d" % (kind, c0), [P, (c1 - c0) * CHUNK], U32, offset)
+                nc.vector.tensor_copy(tile[:], all_words[kind][:].indirect(lists))
+                views = x_words[kind]
+            for c in range(c0, c1):
+                views[c] = (tile, slice((c - c0) * CHUNK, (c - c0 + 1) * CHUNK))
+
         for i, (z, t0, n, nv) in enumerate(X_PIECES):
             grouped = sb("x_bf%d" % i, [P, n * PACK], BF16)
             dst = grouped[:].rearrange("p (c i j) -> p c j i", i=4, j=PACK)
             src = x_raw[i][:].rearrange("p j (c i) -> p c j i", i=4)
-            nc.scalar.copy(dst[:, nv // 4 :], src[:, nv // 4 :])
+            if nv < n:
+                nc.scalar.copy(dst[:, nv // 4 :], src[:, nv // 4 :])
             if nv:
                 nc.vector.tensor_copy(dst[:, : nv // 4], src[:, : nv // 4])
-            for a, b in ((0, nv), (nv, n)) if z == 0 else ((0, n),):
-                cols = slice(t0 + a, t0 + b)
-                nc.vector.quantize_mx(
-                    all_words[z][:, cols].bitcast(FP8X4), all_bytes[4 * z : P, cols], grouped[:, a * PACK : b * PACK]
-                )
+            cols = slice(t0, t0 + n)
+            nc.vector.quantize_mx(all_words[z][:, cols].bitcast(FP8X4), all_bytes[4 * z : P, cols], grouped[:])
             if z == 0 and t0 + n == T:
-                nc.vector.tensor_copy(x_words0[:], all_words[0][:].indirect(offsets[:]))
-        nc.vector.tensor_copy(x_bytes[0][:], all_bytes[:].indirect(offsets[:, : (S - CHUNK) // 16]))
-        nc.vector.tensor_copy(x_words1[0][:], all_words[1][:].indirect(offsets[:, : S // 32]))
+                gather(0, 0, CHUNKS)
+
+        gather("bytes", 0, 3)
 
         def x_operand(z, c):
-            cols = slice(c * CHUNK, (c + 1) * CHUNK)
-            words = x_words0[:, cols] if z == 0 else x_words1[c // 2][:, (c % 2) * CHUNK : (c % 2 + 1) * CHUNK]
-            return dict(rhs=words.bitcast(FP8X4), rhs_scale=x_bytes[0][4 * z : P, cols] if c < CHUNKS - 1 else x_bytes[1][4 * z : P, :])
+            words, word_cols = x_words[z][c]
+            scales, scale_cols = x_bytes[c]
+            return dict(rhs=words[:, word_cols].bitcast(FP8X4), rhs_scale=scales[4 * z : P, scale_cols])
 
         w2_words = [sb("w2_words%d" % z, [P, H], U32) for z in range(PASSES)]
         w2_bytes = [sb("w2_bytes%d" % z, [P, H], U8) for z in range(PASSES)]
-        w_bf = [
-            sb("w_bf0", [P, H * PACK], BF16),
-            late.tile([P, H * PACK], BF16, name="w_bf1", offset=0, align_bytes=64),
-        ]
-        for i, (z, half, mv) in enumerate(W_PIECES):
+        w_bf = [sb("w_bf%d" % z, [P, H * PACK], BF16, offset=4096 * z) for z in range(PASSES)]
+
+        def quantize_w2(z, a, b):
+            nc.vector.quantize_mx(w2_words[z][:, a:b].bitcast(FP8X4), w2_bytes[z][:, a:b], w_bf[z][:, a * PACK : b * PACK])
+
+        def round_w2(i):
+            z, half, mv = W_PIECES[i]
             dst = w_bf[z][:].rearrange("p (t m j) -> p m j t", t=PACK, j=PACK)[:, half * M_HALF : (half + 1) * M_HALF]
             src = w_raw[i][:].rearrange("p j (m t) -> p m j t", t=PACK)
-            nc.scalar.copy(dst[:, mv:], src[:, mv:])
+            if mv < PACK:
+                nc.scalar.copy(dst[:, :, :, mv:], src[:, :, :, mv:])
             if mv:
-                nc.vector.tensor_copy(dst[:, :mv], src[:, :mv])
-            if half == 1:
-                for u in range(2):
-                    cols = slice(u * 2 * P, (u + 1) * 2 * P)
-                    nc.vector.quantize_mx(
-                        w2_words[z][:, cols].bitcast(FP8X4), w2_bytes[z][:, cols],
-                        w_bf[z][:, u * 2 * P * PACK : (u + 1) * 2 * P * PACK],
-                    )
+                nc.vector.tensor_copy(dst[:, :, :, :mv], src[:, :, :, :mv])
 
-        x_words1.append(late.tile([P, S // 2], U32, name="x_words1b", offset=0, align_bytes=64))
-        nc.vector.tensor_copy(x_words1[1][:], all_words[1][:].indirect(offsets[:, S // 32 :]))
-        x_bytes.append(late.tile([P, CHUNK], U8, name="x_bytes_b", offset=1024, align_bytes=64))
-        nc.vector.tensor_copy(x_bytes[1][:], all_bytes[:].indirect(offsets[:, (S - CHUNK) // 16 :]))
+        def quantize_half(z, half):
+            for t in range(PACK):
+                quantize_w2(z, t * P + half * M_HALF, t * P + (half + 1) * M_HALF)
+
+        round_w2(0)
+        round_w2(1)
+        gather(1, 0, 1, offset=8192 + 4096)
+        for u in range(2):
+            quantize_w2(0, u * 2 * P, (u + 1) * 2 * P)
+        gather(1, 1, 3, offset=0)
+        round_w2(2)
+        round_w2(3)
+        quantize_half(1, 0)
+        quantize_half(1, 1)
+        gather(1, 3, 4, offset=4096)
+        gather("bytes", 3, 4, offset=4096 + 1024)
 
         h_banks = [psum.tile([P, PACK, CHUNK], F32, name="h_bank%d" % c, tag="bank%d" % c) for c in range(CHUNKS)]
 
@@ -142,13 +164,14 @@ def tile_picked_lora_gelu_e_kernel(
             for c in range(CHUNKS - 1):
                 h_pass(0, c, (2 * u, 2 * u + 1))
         for c in range(CHUNKS):
-            if c == CHUNKS - 1:
+            if c >= CHUNKS - 1:
                 h_pass(0, c, range(PACK))
             h_pass(1, c, range(PACK))
         for c in range(CHUNKS):
             h_bf = sb("h_bf%d" % c, [P, CHUNK * PACK], BF16)
             nc.scalar.activation(
-                h_bf[:].rearrange("p (n t) -> p n t", t=PACK), h_banks[c][:].rearrange("p t n -> p n t"), GELU
+                h_bf[:].rearrange("p (n t) -> p n t", t=PACK), h_banks[c][:].rearrange("p t n -> p n t"), GELU,
+                bias=zero_bias[:],
             )
             out_bank = psum.tile([P, CHUNK], F32, name="out_bank%d" % c, tag="bank%d" % c)
             for z in range(PASSES):
@@ -164,5 +187,8 @@ def tile_picked_lora_gelu_e_kernel(
                 rhs=h_words[:].bitcast(FP8X4), rhs_scale=h_bytes[:], start=False, stop=True,
             )
             result = sb("result%d" % c, [P, CHUNK], F32)
-            nc.vector.tensor_copy(result[:], out_bank[:])
+            if c in ():
+                nc.scalar.copy(result[:], out_bank[:])
+            else:
+                nc.vector.tensor_copy(result[:], out_bank[:])
             nc.sync.dma_start(out[:, c * CHUNK : (c + 1) * CHUNK], result[:])

@@ -22,7 +22,7 @@ CHUNK = 128
 CHUNKS = S // CHUNK
 LIST_COLS = CHUNK // 16
 
-X_PIECES = ((0, 0, 512, 256), (0, 512, 512, 320), (1, 0, 256, 0), (1, 256, 256, 0), (1, 512, 256, 128), (1, 768, 256, 160))
+X_PIECES = ((0, 0, 512, 256), (0, 512, 256, 0), (0, 768, 256, 128), (1, 0, 256, 0), (1, 256, 256, 0), (1, 512, 256, 64), (1, 768, 256, 160))
 W_PIECES = ((0, 0, 0), (0, 1, 2), (1, 0, 0), (1, 1, 2))
 HALF = H // 2
 M_HALF = HALF // PACK
@@ -142,13 +142,14 @@ def tile_picked_lora_gelu_e_kernel(
         gather(1, 0, 1, offset=8192 + 4096)
         for u in range(2):
             quantize_w2(0, u * 2 * P, (u + 1) * 2 * P)
-        gather(1, 1, 3, offset=0)
         round_w2(2)
         round_w2(3)
         quantize_half(1, 0)
         quantize_half(1, 1)
-        gather(1, 3, 4, offset=4096)
+        gather(1, 1, 2, offset=4096)
         gather("bytes", 3, 4, offset=4096 + 1024)
+        gather(1, 2, 3, offset=4096 + 512)
+        gather(1, 3, 4, offset=4096 + 1536)
 
         h_banks = [psum.tile([P, PACK, CHUNK], F32, name="h_bank%d" % c, tag="bank%d" % c) for c in range(CHUNKS)]
 

@@ -22,7 +22,7 @@ CHUNK = 128
 CHUNKS = S // CHUNK
 LIST_COLS = CHUNK // 16
 
-X_PIECES = ((0, 0, 512, 256), (0, 512, 256, 0), (0, 768, 256, 128), (1, 0, 256, 0), (1, 256, 256, 0), (1, 512, 256, 64), (1, 768, 256, 160))
+X_PIECES = ((0, 0, 512, 256), (0, 512, 256, 0), (0, 768, 256, 96), (1, 0, 256, 0), (1, 256, 256, 0), (1, 512, 256, 0), (1, 768, 256, 160))
 W_PIECES = ((0, 0, 0), (0, 1, 2), (1, 0, 0), (1, 1, 2))
 HALF = H // 2
 M_HALF = HALF // PACK
@@ -111,6 +111,7 @@ def tile_picked_lora_gelu_e_kernel(
                 gather(0, 0, CHUNKS)
 
         gather("bytes", 0, 3)
+        gather(1, 0, 1)
 
         def x_operand(z, c):
             words, word_cols = x_words[z][c]
@@ -139,7 +140,6 @@ def tile_picked_lora_gelu_e_kernel(
 
         round_w2(0)
         round_w2(1)
-        gather(1, 0, 1, offset=8192 + 4096)
         for u in range(2):
             quantize_w2(0, u * 2 * P, (u + 1) * 2 * P)
         round_w2(2)

@@ -13,6 +13,7 @@ U16 = mybir.dt.uint16
 U8 = mybir.dt.uint8
 FP8X4 = mybir.dt.float8_e4m3fn_x4
 GELU = mybir.ActivationFunctionType.Gelu_apprx_tanh
+COPY = mybir.ActivationFunctionType.Copy
 
 P = 128
 PACK = 4
@@ -21,11 +22,7 @@ PASSES = K // K_PASS
 CHUNK = 128
 CHUNKS = S // CHUNK
 LIST_COLS = CHUNK // 16
-
-X_PIECES = ((0, 0, 512, 256), (0, 512, 256, 0), (0, 768, 256, 96), (1, 0, 256, 0), (1, 256, 256, 0), (1, 512, 256, 0), (1, 768, 256, 160))
-W_PIECES = ((0, 0, 0), (0, 1, 2), (1, 0, 0), (1, 1, 2))
-HALF = H // 2
-M_HALF = HALF // PACK
+REST = S - CHUNK
 
 
 def tile_picked_lora_gelu_e_kernel(
@@ -34,41 +31,44 @@ def tile_picked_lora_gelu_e_kernel(
     nc = tc.nc
     with ExitStack() as ctx:
         keep = ctx.enter_context(tc.tile_pool(name="keep", bufs=1))
-        late = ctx.enter_context(tc.tile_pool(name="late", bufs=1))
         psum = ctx.enter_context(tc.psum_pool(name="psum", bufs=1))
 
-        def sb(name, shape, dtype, offset=None):
-            if offset is None:
-                return keep.tile(shape, dtype, name=name, align_bytes=64)
-            return late.tile(shape, dtype, name=name, offset=offset, align_bytes=64)
+        def sb(name, shape, dtype):
+            return keep.tile(shape, dtype, name=name, align_bytes=64)
 
         zeros = sb("zeros", [P, 1], F32)
         zero_bias = sb("zero_bias", [P, 1], F32)
         nc.vector.memset(zeros[:], 0.0)
         nc.scalar.activation(zero_bias[:], zeros[:], GELU)
 
-        all_bytes = sb("all_bytes", [P, T], U8)
         w1_s = sb("w1_s", [P, PASSES, N], U8)
         w3_s = sb("w3_s", [P, N], U8)
         nc.gpsimd.memset(w1_s[:].bitcast(I32), 0)
         nc.vector.memset(w3_s[:].bitcast(I32), 0)
-        nc.vector.memset(all_bytes[:].bitcast(I32), 0)
 
         offsets = keep.tile([P, S // 16], U16, name="offsets")
-        x_raw = []
-        for i, (z, t0, n, nv) in enumerate(X_PIECES):
-            raw = sb("x_raw%d" % i, [P, PACK, n], F32)
-            rows = xT[z * K_PASS : (z + 1) * K_PASS, t0 : t0 + n]
-            nc.sync.dma_start(raw[:], rows.rearrange("(p j) c -> p j c", j=PACK))
-            x_raw.append(raw)
-            if i == 0:
-                nc.sync.dma_start(offsets[:], offs)
-        w_raw = []
-        for i, (z, half, mv) in enumerate(W_PIECES):
-            raw = sb("w_raw%d" % i, [P, PACK, HALF], F32, offset=8192 + 4096 * i)
-            rows = w2[z * K_PASS : (z + 1) * K_PASS, half * HALF : (half + 1) * HALF]
-            nc.sync.dma_start(raw[:], rows.rearrange("(p j) c -> p j c", j=PACK))
-            w_raw.append(raw)
+        planes = {}
+        w_raw = {}
+
+        def load_plane(z, j):
+            planes[z, j] = sb("plane%d_%d" % (z, j), [P, T], F32)
+            rows = xT[z * K_PASS : (z + 1) * K_PASS, :].rearrange("(p j) c -> j p c", j=PACK)
+            nc.sync.dma_start(planes[z, j][:], rows[j])
+
+        def load_w2(z):
+            w_raw[z] = sb("w_raw%d" % z, [P, PACK * H], F32)
+            rows = w2[z * K_PASS : (z + 1) * K_PASS, :].rearrange("(p j) c -> p (j c)", j=PACK)
+            nc.sync.dma_start(w_raw[z][:], rows)
+
+        load_plane(0, 0)
+        nc.sync.dma_start(offsets[:], offs)
+        for j in range(1, PACK):
+            load_plane(0, j)
+        load_w2(1)
+        load_plane(1, 0)
+        load_w2(0)
+        for j in range(1, PACK):
+            load_plane(1, j)
         w1_w = sb("w1_w", [P, PASSES, N], U32)
         w3_w = sb("w3_w", [P, N], U32)
         nc.sync.dma_start(w1_w[:].bitcast(I32), w1_words.rearrange("z p c r -> p z (c r)").bitcast(I32))
@@ -80,116 +80,113 @@ def tile_picked_lora_gelu_e_kernel(
         for r in range(4):
             nc.sync.dma_start(w3_s[r:P:32, :].bitcast(I32), w3_rows[r].bitcast(I32))
 
-        all_words = [sb("all_words%d" % z, [P, T], U32) for z in range(PASSES)]
-        x_words = [[None] * CHUNKS for z in range(PASSES)]
-        x_bytes = [None] * CHUNKS
+        def entries(c0, c1):
+            return offsets[:, c0 * LIST_COLS : c1 * LIST_COLS]
 
-        def gather(kind, c0, c1, offset=None):
-            lists = offsets[:, c0 * LIST_COLS : c1 * LIST_COLS]
-            if kind == "bytes":
-                tile = sb("x_bytes%d" % c0, [P, (c1 - c0) * CHUNK], U8, offset)
-                nc.vector.tensor_copy(tile[:], all_bytes[:].indirect(lists))
-                views = x_bytes
-            else:
-                tile = sb("x_words%d_%d" % (kind, c0), [P, (c1 - c0) * CHUNK], U32, offset)
-                nc.vector.tensor_copy(tile[:], all_words[kind][:].indirect(lists))
-                views = x_words[kind]
+        first_bf = [sb("first_bf%d" % z, [P, CHUNK * PACK], BF16) for z in range(PASSES)]
+        picked = [sb("picked%d" % z, [P, PACK * REST], BF16) for z in range(PASSES)]
+        x_ops = {}
+
+        def gather_first(z, j):
+            dst = first_bf[z][:].rearrange("p (n t) -> p t n", t=PACK)[:, j, :]
+            nc.vector.tensor_copy(dst, planes[z, j][:].indirect(entries(0, 1)))
+
+        def gather_rest(z, j, c0, c1):
+            dst = picked[z][:, j * REST + (c0 - 1) * CHUNK : j * REST + (c1 - 1) * CHUNK]
+            nc.scalar.activation(dst, planes[z, j][:].indirect(entries(c0, c1)), COPY)
+
+        def interleave(z, c0, c1):
+            n = (c1 - c0) * CHUNK
+            grouped = sb("x_bf%d_%d" % (z, c0), [P, n * PACK], BF16)
+            src = picked[z][:].rearrange("p (j n) -> p j n", j=PACK)[:, :, (c0 - 1) * CHUNK : (c1 - 1) * CHUNK]
+            nc.vector.tensor_copy(
+                grouped[:].rearrange("p (c i j) -> p c j i", i=4, j=PACK), src.rearrange("p j (c i) -> p c j i", i=4)
+            )
+            return grouped
+
+        def quantize_x(z, c0, c1, grouped):
+            n = (c1 - c0) * CHUNK
+            words = sb("x_words%d_%d" % (z, c0), [P, n], U32)
+            scales = sb("x_bytes%d_%d" % (z, c0), [P, n], U8)
+            nc.vector.quantize_mx(words[:].bitcast(FP8X4), scales[:], grouped[:])
             for c in range(c0, c1):
-                views[c] = (tile, slice((c - c0) * CHUNK, (c - c0 + 1) * CHUNK))
-
-        for i, (z, t0, n, nv) in enumerate(X_PIECES):
-            grouped = sb("x_bf%d" % i, [P, n * PACK], BF16)
-            dst = grouped[:].rearrange("p (c i j) -> p c j i", i=4, j=PACK)
-            src = x_raw[i][:].rearrange("p j (c i) -> p c j i", i=4)
-            if nv < n:
-                nc.scalar.copy(dst[:, nv // 4 :], src[:, nv // 4 :])
-            if nv:
-                nc.vector.tensor_copy(dst[:, : nv // 4], src[:, : nv // 4])
-            cols = slice(t0, t0 + n)
-            nc.vector.quantize_mx(all_words[z][:, cols].bitcast(FP8X4), all_bytes[4 * z : P, cols], grouped[:])
-            if z == 0 and t0 + n == T:
-                gather(0, 0, CHUNKS)
-
-        gather("bytes", 0, 3)
-        gather(1, 0, 1)
-
-        def x_operand(z, c):
-            words, word_cols = x_words[z][c]
-            scales, scale_cols = x_bytes[c]
-            return dict(rhs=words[:, word_cols].bitcast(FP8X4), rhs_scale=scales[4 * z : P, scale_cols])
+                cols = slice((c - c0) * CHUNK, (c - c0 + 1) * CHUNK)
+                x_ops[z, c] = dict(rhs=words[:, cols].bitcast(FP8X4), rhs_scale=scales[:, cols])
 
         w2_words = [sb("w2_words%d" % z, [P, H], U32) for z in range(PASSES)]
         w2_bytes = [sb("w2_bytes%d" % z, [P, H], U8) for z in range(PASSES)]
-        w_bf = [sb("w_bf%d" % z, [P, H * PACK], BF16, offset=4096 * z) for z in range(PASSES)]
+        w_bf = [sb("w_bf%d" % z, [P, H * PACK], BF16) for z in range(PASSES)]
 
-        def quantize_w2(z, a, b):
+        def round_w2(z, engine_copy, t0, t1):
+            dst = w_bf[z][:].rearrange("p (t m j) -> p m j t", t=PACK, j=PACK)
+            src = w_raw[z][:].rearrange("p (j m t) -> p m j t", j=PACK, t=PACK)
+            engine_copy(dst[:, :, :, t0:t1], src[:, :, :, t0:t1])
+
+        def quantize_w2(z, t0, t1):
+            a, b = t0 * P, t1 * P
             nc.vector.quantize_mx(w2_words[z][:, a:b].bitcast(FP8X4), w2_bytes[z][:, a:b], w_bf[z][:, a * PACK : b * PACK])
 
-        def round_w2(i):
-            z, half, mv = W_PIECES[i]
-            dst = w_bf[z][:].rearrange("p (t m j) -> p m j t", t=PACK, j=PACK)[:, half * M_HALF : (half + 1) * M_HALF]
-            src = w_raw[i][:].rearrange("p j (m t) -> p m j t", t=PACK)
-            if mv < PACK:
-                nc.scalar.copy(dst[:, :, :, mv:], src[:, :, :, mv:])
-            if mv:
-                nc.vector.tensor_copy(dst[:, :, :, :mv], src[:, :, :, :mv])
-
-        def quantize_half(z, half):
-            for t in range(PACK):
-                quantize_w2(z, t * P + half * M_HALF, t * P + (half + 1) * M_HALF)
-
-        round_w2(0)
-        round_w2(1)
-        for u in range(2):
-            quantize_w2(0, u * 2 * P, (u + 1) * 2 * P)
-        round_w2(2)
-        round_w2(3)
-        quantize_half(1, 0)
-        quantize_half(1, 1)
-        gather(1, 1, 2, offset=4096)
-        gather("bytes", 3, 4, offset=4096 + 1024)
-        gather(1, 2, 3, offset=4096 + 512)
-        gather(1, 3, 4, offset=4096 + 1536)
-
-        h_banks = [psum.tile([P, PACK, CHUNK], F32, name="h_bank%d" % c, tag="bank%d" % c) for c in range(CHUNKS)]
+        h_banks = [psum.tile([P, PACK, CHUNK], F32, name="h_bank%d" % c) for c in range(CHUNKS)]
+        out_banks = [psum.tile([P, CHUNK], F32, name="out_bank%d" % c) for c in range(CHUNKS)]
 
         def h_pass(z, c, ts):
             for t in ts:
                 cols = slice(t * P, (t + 1) * P)
                 nc.tensor.matmul_mx(
                     h_banks[c][:, t, :], lhsT=w2_words[z][:, cols].bitcast(FP8X4), lhsT_scale=w2_bytes[z][:, cols],
-                    start=(z == 0 and t == 0), stop=(z == PASSES - 1 and t == PACK - 1), **x_operand(z, c)
+                    start=(z == 0 and t == 0), stop=(z == PASSES - 1 and t == PACK - 1), **x_ops[z, c]
                 )
 
+        for j in range(PACK):
+            gather_first(0, j)
+            gather_rest(0, j, 1, CHUNKS)
+        rest0 = interleave(0, 1, CHUNKS)
+        quantize_x(0, 0, 1, first_bf[0])
+        round_w2(1, nc.vector.tensor_copy, 0, 2)
+        quantize_x(0, 1, CHUNKS, rest0)
+        round_w2(1, nc.vector.tensor_copy, 2, 4)
+        gather_first(1, 0)
+        gather_rest(1, 0, 1, CHUNKS)
+        quantize_w2(1, 0, 4)
+        round_w2(0, nc.vector.tensor_copy, 0, 2)
+        round_w2(0, nc.scalar.copy, 2, 4)
+        quantize_w2(0, 0, 2)
+        gather_first(1, 1)
+        gather_rest(1, 1, 1, CHUNKS)
+        quantize_w2(0, 2, 4)
         for u in range(2):
-            for c in range(CHUNKS - 1):
+            for c in range(CHUNKS):
                 h_pass(0, c, (2 * u, 2 * u + 1))
+        gather_first(1, 2)
+        gather_rest(1, 2, 1, CHUNKS)
+        gather_first(1, 3)
+        for c in range(1, CHUNKS):
+            gather_rest(1, 3, c, c + 1)
+        grouped = first_bf[1]
         for c in range(CHUNKS):
-            if c >= CHUNKS - 1:
-                h_pass(0, c, range(PACK))
+            ahead = interleave(1, c + 1, c + 2) if c + 1 < CHUNKS else None
+            quantize_x(1, c, c + 1, grouped)
             h_pass(1, c, range(PACK))
+            grouped = ahead
+
         for c in range(CHUNKS):
             h_bf = sb("h_bf%d" % c, [P, CHUNK * PACK], BF16)
             nc.scalar.activation(
                 h_bf[:].rearrange("p (n t) -> p n t", t=PACK), h_banks[c][:].rearrange("p t n -> p n t"), GELU,
                 bias=zero_bias[:],
             )
-            out_bank = psum.tile([P, CHUNK], F32, name="out_bank%d" % c, tag="bank%d" % c)
             for z in range(PASSES):
                 nc.tensor.matmul_mx(
-                    out_bank[:], lhsT=w1_w[:, z, :].bitcast(FP8X4), lhsT_scale=w1_s[:, z, :],
-                    start=(z == 0), stop=False, **x_operand(z, c)
+                    out_banks[c][:], lhsT=w1_w[:, z, :].bitcast(FP8X4), lhsT_scale=w1_s[:, z, :],
+                    start=(z == 0), stop=False, **x_ops[z, c]
                 )
             h_words = sb("h_words%d" % c, [P, CHUNK], U32)
             h_bytes = sb("h_bytes%d" % c, [P, CHUNK], U8)
             nc.vector.quantize_mx(h_words[:].bitcast(FP8X4), h_bytes[:], h_bf[:])
             nc.tensor.matmul_mx(
-                out_bank[:], lhsT=w3_w[:].bitcast(FP8X4), lhsT_scale=w3_s[:],
+                out_banks[c][:], lhsT=w3_w[:].bitcast(FP8X4), lhsT_scale=w3_s[:],
                 rhs=h_words[:].bitcast(FP8X4), rhs_scale=h_bytes[:], start=False, stop=True,
             )
             result = sb("result%d" % c, [P, CHUNK], F32)
-            if c in ():
-                nc.scalar.copy(result[:], out_bank[:])
-            else:
-                nc.vector.tensor_copy(result[:], out_bank[:])
+            nc.vector.tensor_copy(result[:], out_banks[c][:])
             nc.sync.dma_start(out[:, c * CHUNK : (c + 1) * CHUNK], result[:])

@@ -83,26 +83,24 @@ def tile_picked_lora_gelu_e_kernel(
         def entries(c0, c1):
             return offsets[:, c0 * LIST_COLS : c1 * LIST_COLS]
 
-        first_bf = [sb("first_bf%d" % z, [P, CHUNK * PACK], BF16) for z in range(PASSES)]
         picked = [sb("picked%d" % z, [P, PACK * REST], BF16) for z in range(PASSES)]
+        first_bf0 = sb("first_bf0", [P, CHUNK * PACK], BF16)
+        rest_bf0 = sb("rest_bf0", [P, REST * PACK], BF16)
+        x_bf1 = [sb("x_bf1_%d" % c, [P, CHUNK * PACK], BF16) for c in range(CHUNKS)]
         x_ops = {}
 
-        def gather_first(z, j):
-            dst = first_bf[z][:].rearrange("p (n t) -> p t n", t=PACK)[:, j, :]
-            nc.vector.tensor_copy(dst, planes[z, j][:].indirect(entries(0, 1)))
+        def gather_first(j, z=1, c=0):
+            dst = (first_bf0, x_bf1[c])[z][:].rearrange("p (n t) -> p t n", t=PACK)[:, j, :]
+            nc.vector.tensor_copy(dst, planes[z, j][:].indirect(entries(c, c + 1)))
 
-        def gather_rest(z, j, c0, c1):
+        def gather_rest(j, c0, c1, z=1):
             dst = picked[z][:, j * REST + (c0 - 1) * CHUNK : j * REST + (c1 - 1) * CHUNK]
             nc.scalar.activation(dst, planes[z, j][:].indirect(entries(c0, c1)), COPY)
 
-        def interleave(z, c0, c1):
-            n = (c1 - c0) * CHUNK
-            grouped = sb("x_bf%d_%d" % (z, c0), [P, n * PACK], BF16)
-            src = picked[z][:].rearrange("p (j n) -> p j n", j=PACK)[:, :, (c0 - 1) * CHUNK : (c1 - 1) * CHUNK]
-            nc.vector.tensor_copy(
-                grouped[:].rearrange("p (c i j) -> p c j i", i=4, j=PACK), src.rearrange("p j (c i) -> p c j i", i=4)
-            )
-            return grouped
+        def interleave_planes(j0, j1, c):
+            src = picked[1][:].rearrange("p (j n) -> p j n", j=PACK)[:, j0:j1, (c - 1) * CHUNK : c * CHUNK]
+            dst = x_bf1[c][:].rearrange("p (c i j) -> p c j i", i=2, j=PACK)[:, :, j0:j1, :]
+            nc.vector.tensor_copy(dst, src.rearrange("p j (c i) -> p c j i", i=2))
 
         def quantize_x(z, c0, c1, grouped):
             n = (c1 - c0) * CHUNK
@@ -138,36 +136,45 @@ def tile_picked_lora_gelu_e_kernel(
                 )
 
         for j in range(PACK):
-            gather_first(0, j)
-            gather_rest(0, j, 1, CHUNKS)
-        rest0 = interleave(0, 1, CHUNKS)
-        quantize_x(0, 0, 1, first_bf[0])
+            gather_first(j, 0)
+            gather_rest(j, 1, CHUNKS, 0)
+        nc.vector.tensor_copy(
+            rest_bf0[:].rearrange("p (c i j) -> p c j i", i=4, j=PACK),
+            picked[0][:].rearrange("p (j c i) -> p c j i", i=4, j=PACK),
+        )
+        quantize_x(0, 0, 1, first_bf0)
         round_w2(1, nc.vector.tensor_copy, 0, 2)
-        quantize_x(0, 1, CHUNKS, rest0)
         round_w2(1, nc.vector.tensor_copy, 2, 4)
-        gather_first(1, 0)
-        gather_rest(1, 0, 1, CHUNKS)
+        quantize_x(0, 1, CHUNKS, rest_bf0)
+        gather_first(0)
+        gather_rest(0, 1, CHUNKS)
         quantize_w2(1, 0, 4)
         round_w2(0, nc.vector.tensor_copy, 0, 2)
         round_w2(0, nc.scalar.copy, 2, 4)
         quantize_w2(0, 0, 2)
-        gather_first(1, 1)
-        gather_rest(1, 1, 1, CHUNKS)
+        gather_first(1)
+        gather_rest(1, 1, CHUNKS)
         quantize_w2(0, 2, 4)
         for u in range(2):
             for c in range(CHUNKS):
                 h_pass(0, c, (2 * u, 2 * u + 1))
-        gather_first(1, 2)
-        gather_rest(1, 2, 1, CHUNKS)
-        gather_first(1, 3)
-        for c in range(1, CHUNKS):
-            gather_rest(1, 3, c, c + 1)
-        grouped = first_bf[1]
-        for c in range(CHUNKS):
-            ahead = interleave(1, c + 1, c + 2) if c + 1 < CHUNKS else None
-            quantize_x(1, c, c + 1, grouped)
+        for c in range(2, CHUNKS):
+            interleave_planes(0, 2, c)
+        gather_first(2)
+        gather_rest(2, 1, 2)
+        gather_rest(2, 2, CHUNKS)
+        interleave_planes(0, 3, 1)
+        gather_first(3)
+        gather_first(3, c=1)
+        gather_rest(3, 2, CHUNKS)
+        for c in range(2):
+            quantize_x(1, c, c + 1, x_bf1[c])
             h_pass(1, c, range(PACK))
-            grouped = ahead
+        for c in range(2, CHUNKS):
+            interleave_planes(2, 4, c)
+        for c in range(2, CHUNKS):
+            quantize_x(1, c, c + 1, x_bf1[c])
+            h_pass(1, c, range(PACK))
 
         for c in range(CHUNKS):
             h_bf = sb("h_bf%d" % c, [P, CHUNK * PACK], BF16)

@@ -51,19 +51,25 @@ def tile_picked_lora_gelu_e_kernel(
         w_raw = {}
 
         def load_plane(z, j):
-            planes[z, j] = sb("plane%d_%d" % (z, j), [P, T], F32)
+            planes[z, j] = sb("plane%d_%d" % (z, j), [P, T], F32)[:]
             rows = xT[z * K_PASS : (z + 1) * K_PASS, :].rearrange("(p j) c -> j p c", j=PACK)
-            nc.sync.dma_start(planes[z, j][:], rows[j])
+            nc.sync.dma_start(planes[z, j], rows[j])
+
+        def load_plane_pair(z, j):
+            pair = sb("pair%d_%d" % (z, j), [P, 2 * T], F32)
+            rows = xT[z * K_PASS : (z + 1) * K_PASS, :].rearrange("(p u j) c -> u p (j c)", u=2, j=2)
+            nc.sync.dma_start(pair[:], rows[j // 2])
+            planes[z, j] = pair[:, :T]
+            planes[z, j + 1] = pair[:, T:]
 
         def load_w2(z):
             w_raw[z] = sb("w_raw%d" % z, [P, PACK * H], F32)
             rows = w2[z * K_PASS : (z + 1) * K_PASS, :].rearrange("(p j) c -> p (j c)", j=PACK)
             nc.sync.dma_start(w_raw[z][:], rows)
 
-        load_plane(0, 0)
+        load_plane_pair(0, 0)
         nc.sync.dma_start(offsets[:], offs)
-        for j in range(1, PACK):
-            load_plane(0, j)
+        load_plane_pair(0, 2)
         load_w2(1)
         load_plane(1, 0)
         load_w2(0)
@@ -74,7 +80,7 @@ def tile_picked_lora_gelu_e_kernel(
         nc.sync.dma_start(w1_w[:].bitcast(I32), w1_words.rearrange("z p c r -> p z (c r)").bitcast(I32))
         w1_rows = w1_scales.rearrange("z (q r) c -> r q z c", r=4)
         for r in range(4):
-            nc.gpsimd.dma_start(w1_s[r:P:32, :, :].bitcast(I32), w1_rows[r].bitcast(I32))
+            nc.sync.dma_start(w1_s[r:P:32, :, :].bitcast(I32), w1_rows[r].bitcast(I32))
         nc.sync.dma_start(w3_w[:].bitcast(I32), w3_words[0].rearrange("p c r -> p (c r)").bitcast(I32))
         w3_rows = w3_scales[0].rearrange("(q r) c -> r q c", r=4)
         for r in range(4):
@@ -83,7 +89,7 @@ def tile_picked_lora_gelu_e_kernel(
         def entries(c0, c1):
             return offsets[:, c0 * LIST_COLS : c1 * LIST_COLS]
 
-        picked = [sb("picked%d" % z, [P, PACK * REST], BF16) for z in range(PASSES)]
+        picked = [sb("picked%d" % z, [P, PACK * REST], (F32, BF16)[z]) for z in range(PASSES)]
         first_bf0 = sb("first_bf0", [P, CHUNK * PACK], BF16)
         rest_bf0 = sb("rest_bf0", [P, REST * PACK], BF16)
         x_bf1 = [sb("x_bf1_%d" % c, [P, CHUNK * PACK], BF16) for c in range(CHUNKS)]
@@ -91,11 +97,11 @@ def tile_picked_lora_gelu_e_kernel(
 
         def gather_first(j, z=1, c=0):
             dst = (first_bf0, x_bf1[c])[z][:].rearrange("p (n t) -> p t n", t=PACK)[:, j, :]
-            nc.vector.tensor_copy(dst, planes[z, j][:].indirect(entries(c, c + 1)))
+            nc.vector.tensor_copy(dst, planes[z, j].indirect(entries(c, c + 1)))
 
         def gather_rest(j, c0, c1, z=1):
             dst = picked[z][:, j * REST + (c0 - 1) * CHUNK : j * REST + (c1 - 1) * CHUNK]
-            nc.scalar.activation(dst, planes[z, j][:].indirect(entries(c0, c1)), COPY)
+            nc.scalar.activation(dst, planes[z, j].indirect(entries(c0, c1)), COPY)
 
         def interleave_planes(j0, j1, c):
             src = picked[1][:].rearrange("p (j n) -> p j n", j=PACK)[:, j0:j1, (c - 1) * CHUNK : c * CHUNK]
@@ -144,7 +150,7 @@ def tile_picked_lora_gelu_e_kernel(
         )
         quantize_x(0, 0, 1, first_bf0)
         round_w2(1, nc.vector.tensor_copy, 0, 2)
-        round_w2(1, nc.vector.tensor_copy, 2, 4)
+        round_w2(1, nc.scalar.copy, 2, 4)
         quantize_x(0, 1, CHUNKS, rest_bf0)
         gather_first(0)
         gather_rest(0, 1, CHUNKS)

@@ -130,15 +130,16 @@ def tile_picked_lora_gelu_e_kernel(
             a, b = t0 * P, t1 * P
             nc.vector.quantize_mx(w2_words[z][:, a:b].bitcast(FP8X4), w2_bytes[z][:, a:b], w_bf[z][:, a * PACK : b * PACK])
 
-        h_banks = [psum.tile([P, PACK, CHUNK], F32, name="h_bank%d" % c) for c in range(CHUNKS)]
-        out_banks = [psum.tile([P, CHUNK], F32, name="out_bank%d" % c) for c in range(CHUNKS)]
+        first_banks = [psum.tile([P, 2, CHUNK], F32, name="first_bank%d" % u, tag="first%d" % u) for u in range(2)]
+        h_banks = {c: psum.tile([P, PACK, CHUNK], F32, name="h_bank%d" % c) for c in range(1, CHUNKS)}
 
         def h_pass(z, c, ts):
             for t in ts:
                 cols = slice(t * P, (t + 1) * P)
+                bank, slot, slots = (first_banks[t // 2], t % 2, 2) if c == 0 else (h_banks[c], t, PACK)
                 nc.tensor.matmul_mx(
-                    h_banks[c][:, t, :], lhsT=w2_words[z][:, cols].bitcast(FP8X4), lhsT_scale=w2_bytes[z][:, cols],
-                    start=(z == 0 and t == 0), stop=(z == PASSES - 1 and t == PACK - 1), **x_ops[z, c]
+                    bank[:, slot, :], lhsT=w2_words[z][:, cols].bitcast(FP8X4), lhsT_scale=w2_bytes[z][:, cols],
+                    start=(z == 0 and slot == 0), stop=(z == PASSES - 1 and slot == slots - 1), **x_ops[z, c]
                 )
 
         for j in range(PACK):
@@ -184,22 +185,36 @@ def tile_picked_lora_gelu_e_kernel(
 
         for c in range(CHUNKS):
             h_bf = sb("h_bf%d" % c, [P, CHUNK * PACK], BF16)
-            nc.scalar.activation(
-                h_bf[:].rearrange("p (n t) -> p n t", t=PACK), h_banks[c][:].rearrange("p t n -> p n t"), GELU,
-                bias=zero_bias[:],
-            )
+            if c == 0:
+                pairs = sb("h_pairs", [P, 2, 2 * CHUNK], BF16)
+                for u in range(2):
+                    nc.scalar.activation(
+                        pairs[:, u, :].rearrange("p (n t) -> p n t", t=2), first_banks[u][:].rearrange("p t n -> p n t"), GELU
+                    )
+                nc.vector.tensor_copy(
+                    h_bf[:].bitcast(I32).rearrange("p (n u) -> p n u", u=2), pairs[:].bitcast(I32).rearrange("p u n -> p n u")
+                )
+            else:
+                nc.scalar.activation(
+                    h_bf[:].rearrange("p (n t) -> p n t", t=PACK), h_banks[c][:].rearrange("p t n -> p n t"), GELU,
+                    bias=(zero_bias[:] if c == 1 else 0.0),
+                )
+            out_bank = psum.tile([P, CHUNK], F32, name="out_bank%d" % c, tag=("first0" if c == CHUNKS - 1 else "out%d" % c))
             for z in range(PASSES):
                 nc.tensor.matmul_mx(
-                    out_banks[c][:], lhsT=w1_w[:, z, :].bitcast(FP8X4), lhsT_scale=w1_s[:, z, :],
+                    out_bank[:], lhsT=w1_w[:, z, :].bitcast(FP8X4), lhsT_scale=w1_s[:, z, :],
                     start=(z == 0), stop=False, **x_ops[z, c]
                 )
             h_words = sb("h_words%d" % c, [P, CHUNK], U32)
             h_bytes = sb("h_bytes%d" % c, [P, CHUNK], U8)
             nc.vector.quantize_mx(h_words[:].bitcast(FP8X4), h_bytes[:], h_bf[:])
             nc.tensor.matmul_mx(
-                out_banks[c][:], lhsT=w3_w[:].bitcast(FP8X4), lhsT_scale=w3_s[:],
+                out_bank[:], lhsT=w3_w[:].bitcast(FP8X4), lhsT_scale=w3_s[:],
                 rhs=h_words[:].bitcast(FP8X4), rhs_scale=h_bytes[:], start=False, stop=True,
             )
             result = sb("result%d" % c, [P, CHUNK], F32)
-            nc.vector.tensor_copy(result[:], out_banks[c][:])
+            if c == CHUNKS - 1:
+                nc.scalar.copy(result[:], out_bank[:])
+            else:
+                nc.vector.tensor_copy(result[:], out_bank[:])
             nc.sync.dma_start(out[:, c * CHUNK : (c + 1) * CHUNK], result[:])

@@ -105,8 +105,8 @@ def tile_picked_lora_gelu_e_kernel(
 
         def interleave_planes(j0, j1, c):
             src = picked[1][:].rearrange("p (j n) -> p j n", j=PACK)[:, j0:j1, (c - 1) * CHUNK : c * CHUNK]
-            dst = x_bf1[c][:].rearrange("p (c i j) -> p c j i", i=2, j=PACK)[:, :, j0:j1, :]
-            nc.vector.tensor_copy(dst, src.rearrange("p j (c i) -> p c j i", i=2))
+            dst = x_bf1[c][:].rearrange("p (c i j) -> p c j i", i=4, j=PACK)[:, :, j0:j1, :]
+            nc.vector.tensor_copy(dst, src.rearrange("p j (c i) -> p c j i", i=4))
 
         def quantize_x(z, c0, c1, grouped):
             n = (c1 - c0) * CHUNK
@@ -165,8 +165,6 @@ def tile_picked_lora_gelu_e_kernel(
         for u in range(2):
             for c in range(CHUNKS):
                 h_pass(0, c, (2 * u, 2 * u + 1))
-        for c in range(2, CHUNKS):
-            interleave_planes(0, 2, c)
         gather_first(2)
         gather_rest(2, 1, 2)
         gather_rest(2, 2, CHUNKS)
@@ -178,7 +176,7 @@ def tile_picked_lora_gelu_e_kernel(
             quantize_x(1, c, c + 1, x_bf1[c])
             h_pass(1, c, range(PACK))
         for c in range(2, CHUNKS):
-            interleave_planes(2, 4, c)
+            interleave_planes(0, 4, c)
         for c in range(2, CHUNKS):
             quantize_x(1, c, c + 1, x_bf1[c])
             h_pass(1, c, range(PACK))

@@ -183,6 +183,7 @@ def tile_picked_lora_gelu_e_kernel(
 
         for c in range(CHUNKS):
             h_bf = sb("h_bf%d" % c, [P, CHUNK * PACK], BF16)
+            halves = ((0, CHUNK // 2), (CHUNK // 2, CHUNK)) if c == CHUNKS - 1 else ((0, CHUNK),)
             if c == 0:
                 pairs = sb("h_pairs", [P, 2, 2 * CHUNK], BF16)
                 for u in range(2):
@@ -193,10 +194,12 @@ def tile_picked_lora_gelu_e_kernel(
                     h_bf[:].bitcast(I32).rearrange("p (n u) -> p n u", u=2), pairs[:].bitcast(I32).rearrange("p u n -> p n u")
                 )
             else:
-                nc.scalar.activation(
-                    h_bf[:].rearrange("p (n t) -> p n t", t=PACK), h_banks[c][:].rearrange("p t n -> p n t"), GELU,
-                    bias=(zero_bias[:] if c == 1 else 0.0),
-                )
+                for a, b in halves:
+                    nc.scalar.activation(
+                        h_bf[:, a * PACK : b * PACK].rearrange("p (n t) -> p n t", t=PACK),
+                        h_banks[c][:, :, a:b].rearrange("p t n -> p n t"), GELU,
+                        bias=(zero_bias[:] if c == 1 else 0.0),
+                    )
             out_bank = psum.tile([P, CHUNK], F32, name="out_bank%d" % c, tag=("first0" if c == CHUNKS - 1 else "out%d" % c))
             for z in range(PASSES):
                 nc.tensor.matmul_mx(
@@ -205,13 +208,14 @@ def tile_picked_lora_gelu_e_kernel(
                 )
             h_words = sb("h_words%d" % c, [P, CHUNK], U32)
             h_bytes = sb("h_bytes%d" % c, [P, CHUNK], U8)
-            nc.vector.quantize_mx(h_words[:].bitcast(FP8X4), h_bytes[:], h_bf[:])
+            for a, b in halves:
+                nc.vector.quantize_mx(h_words[:, a:b].bitcast(FP8X4), h_bytes[:, a:b], h_bf[:, a * PACK : b * PACK])
             nc.tensor.matmul_mx(
                 out_bank[:], lhsT=w3_w[:].bitcast(FP8X4), lhsT_scale=w3_s[:],
                 rhs=h_words[:].bitcast(FP8X4), rhs_scale=h_bytes[:], start=False, stop=True,
             )
             result = sb("result%d" % c, [P, CHUNK], F32)
-            if c == CHUNKS - 1:
+            if c > 0:
                 nc.scalar.copy(result[:], out_bank[:])
             else:
                 nc.vector.tensor_copy(result[:], out_bank[:])

@@ -34,7 +34,7 @@ def tile_picked_lora_gelu_e_kernel(
         psum = ctx.enter_context(tc.psum_pool(name="psum", bufs=1))
 
         def sb(name, shape, dtype):
-            return keep.tile(shape, dtype, name=name, align_bytes=64)
+            return keep.tile(shape, dtype, name=name, align_bytes=256)
 
         zeros = sb("zeros", [P, 1], F32)
         zero_bias = sb("zero_bias", [P, 1], F32)

@@ -33,8 +33,8 @@ def tile_picked_lora_gelu_e_kernel(
         keep = ctx.enter_context(tc.tile_pool(name="keep", bufs=1))
         psum = ctx.enter_context(tc.psum_pool(name="psum", bufs=1))
 
-        def sb(name, shape, dtype):
-            return keep.tile(shape, dtype, name=name, align_bytes=256)
+        def sb(name, shape, dtype, align=256):
+            return keep.tile(shape, dtype, name=name, align_bytes=align)
 
         zeros = sb("zeros", [P, 1], F32)
         zero_bias = sb("zero_bias", [P, 1], F32)
@@ -51,19 +51,19 @@ def tile_picked_lora_gelu_e_kernel(
         w_raw = {}
 
         def load_plane(z, j):
-            planes[z, j] = sb("plane%d_%d" % (z, j), [P, T], F32)[:]
+            planes[z, j] = sb("plane%d_%d" % (z, j), [P, T], F32, 4096)[:]
             rows = xT[z * K_PASS : (z + 1) * K_PASS, :].rearrange("(p j) c -> j p c", j=PACK)
             nc.sync.dma_start(planes[z, j], rows[j])
 
         def load_plane_pair(z, j):
-            pair = sb("pair%d_%d" % (z, j), [P, 2 * T], F32)
+            pair = sb("pair%d_%d" % (z, j), [P, 2 * T], F32, 4096)
             rows = xT[z * K_PASS : (z + 1) * K_PASS, :].rearrange("(p u j) c -> u p (j c)", u=2, j=2)
             nc.sync.dma_start(pair[:], rows[j // 2])
             planes[z, j] = pair[:, :T]
             planes[z, j + 1] = pair[:, T:]
 
         def load_w2(z):
-            w_raw[z] = sb("w_raw%d" % z, [P, PACK * H], F32)
+            w_raw[z] = sb("w_raw%d" % z, [P, PACK * H], F32, 4096)
             rows = w2[z * K_PASS : (z + 1) * K_PASS, :].rearrange("(p j) c -> p (j c)", j=PACK)
             nc.sync.dma_start(w_raw[z][:], rows)
 

@@ -33,9 +33,20 @@ def tile_picked_lora_gelu_e_kernel(
         keep = ctx.enter_context(tc.tile_pool(name="keep", bufs=1))
         psum = ctx.enter_context(tc.psum_pool(name="psum", bufs=1))
 
-        def sb(name, shape, dtype, align=256):
-            return keep.tile(shape, dtype, name=name, align_bytes=align)
+        def sb(name, shape, dtype, align=256, tag=None):
+            return keep.tile(shape, dtype, name=name, tag=tag or name, align_bytes=align)
 
+        planes = {}
+
+        def load_plane_pair(z, j, queue=nc.sync):
+            pair = sb("pair%d_%d" % (z, j), [P, 2 * T], F32, 4096)
+            rows = xT[z * K_PASS : (z + 1) * K_PASS, :].rearrange("(p u j) c -> u p (j c)", u=2, j=2)
+            queue.dma_start(pair[:], rows[j // 2])
+            planes[z, j] = pair[:, :T]
+            planes[z, j + 1] = pair[:, T:]
+
+        planes[1, 0] = sb("plane1_0", [P, T], F32, 4096)[:]
+        nc.scalar.dma_start(planes[1, 0], xT[K_PASS:, :].rearrange("(p j) c -> j p c", j=PACK)[0])
         zeros = sb("zeros", [P, 1], F32)
         zero_bias = sb("zero_bias", [P, 1], F32)
         nc.vector.memset(zeros[:], 0.0)
@@ -47,7 +58,6 @@ def tile_picked_lora_gelu_e_kernel(
         nc.vector.memset(w3_s[:].bitcast(I32), 0)
 
         offsets = keep.tile([P, S // 16], U16, name="offsets")
-        planes = {}
         w_raw = {}
 
         def load_plane(z, j):
@@ -55,24 +65,16 @@ def tile_picked_lora_gelu_e_kernel(
             rows = xT[z * K_PASS : (z + 1) * K_PASS, :].rearrange("(p j) c -> j p c", j=PACK)
             nc.sync.dma_start(planes[z, j], rows[j])
 
-        def load_plane_pair(z, j):
-            pair = sb("pair%d_%d" % (z, j), [P, 2 * T], F32, 4096)
-            rows = xT[z * K_PASS : (z + 1) * K_PASS, :].rearrange("(p u j) c -> u p (j c)", u=2, j=2)
-            nc.sync.dma_start(pair[:], rows[j // 2])
-            planes[z, j] = pair[:, :T]
-            planes[z, j + 1] = pair[:, T:]
-
         def load_w2(z):
             w_raw[z] = sb("w_raw%d" % z, [P, PACK * H], F32, 4096)
             rows = w2[z * K_PASS : (z + 1) * K_PASS, :].rearrange("(p j) c -> p (j c)", j=PACK)
             nc.sync.dma_start(w_raw[z][:], rows)
 
-        load_plane_pair(0, 0)
         nc.sync.dma_start(offsets[:], offs)
+        load_plane_pair(0, 0)
         load_plane_pair(0, 2)
-        load_w2(1)
-        load_plane(1, 0)
         load_w2(0)
+        load_w2(1)
         for j in range(1, PACK):
             load_plane(1, j)
         w1_w = sb("w1_w", [P, PASSES, N], U32)
@@ -117,8 +119,7 @@ def tile_picked_lora_gelu_e_kernel(
                 cols = slice((c - c0) * CHUNK, (c - c0 + 1) * CHUNK)
                 x_ops[z, c] = dict(rhs=words[:, cols].bitcast(FP8X4), rhs_scale=scales[:, cols])
 
-        w2_words = [sb("w2_words%d" % z, [P, H], U32) for z in range(PASSES)]
-        w2_bytes = [sb("w2_bytes%d" % z, [P, H], U8) for z in range(PASSES)]
+        w_ops = {}
         w_bf = [sb("w_bf%d" % z, [P, H * PACK], BF16) for z in range(PASSES)]
 
         def round_w2(z, engine_copy, t0, t1):
@@ -126,42 +127,47 @@ def tile_picked_lora_gelu_e_kernel(
             src = w_raw[z][:].rearrange("p (j m t) -> p m j t", j=PACK, t=PACK)
             engine_copy(dst[:, :, :, t0:t1], src[:, :, :, t0:t1])
 
-        def quantize_w2(z, t0, t1):
-            a, b = t0 * P, t1 * P
-            nc.vector.quantize_mx(w2_words[z][:, a:b].bitcast(FP8X4), w2_bytes[z][:, a:b], w_bf[z][:, a * PACK : b * PACK])
+        def quantize_w2(z, t0, t1, align=256, tag=None):
+            n = (t1 - t0) * P
+            words = sb("w2_words%d_%d" % (z, t0), [P, n], U32, align, tag)
+            scales = sb("w2_bytes%d_%d" % (z, t0), [P, n], U8)
+            nc.vector.quantize_mx(words[:].bitcast(FP8X4), scales[:], w_bf[z][:, t0 * P * PACK : t1 * P * PACK])
+            for t in range(t0, t1):
+                cols = slice((t - t0) * P, (t - t0 + 1) * P)
+                w_ops[z, t] = dict(lhsT=words[:, cols].bitcast(FP8X4), lhsT_scale=scales[:, cols])
 
         first_banks = [psum.tile([P, 2, CHUNK], F32, name="first_bank%d" % u, tag="first%d" % u) for u in range(2)]
         h_banks = {c: psum.tile([P, PACK, CHUNK], F32, name="h_bank%d" % c) for c in range(1, CHUNKS)}
 
         def h_pass(z, c, ts):
             for t in ts:
-                cols = slice(t * P, (t + 1) * P)
                 bank, slot, slots = (first_banks[t // 2], t % 2, 2) if c == 0 else (h_banks[c], t, PACK)
                 nc.tensor.matmul_mx(
-                    bank[:, slot, :], lhsT=w2_words[z][:, cols].bitcast(FP8X4), lhsT_scale=w2_bytes[z][:, cols],
-                    start=(z == 0 and slot == 0), stop=(z == PASSES - 1 and slot == slots - 1), **x_ops[z, c]
+                    bank[:, slot, :],
+                    start=(z == 0 and slot == 0), stop=(z == PASSES - 1 and slot == slots - 1), **w_ops[z, t], **x_ops[z, c]
                 )
 
-        for j in range(PACK):
-            gather_first(j, 0)
-            gather_rest(j, 1, CHUNKS, 0)
-        nc.vector.tensor_copy(
-            rest_bf0[:].rearrange("p (c i j) -> p c j i", i=4, j=PACK),
-            picked[0][:].rearrange("p (j c i) -> p c j i", i=4, j=PACK),
-        )
-        quantize_x(0, 0, 1, first_bf0)
-        round_w2(1, nc.vector.tensor_copy, 0, 2)
-        round_w2(1, nc.scalar.copy, 2, 4)
-        quantize_x(0, 1, CHUNKS, rest_bf0)
         gather_first(0)
         gather_rest(0, 1, CHUNKS)
-        quantize_w2(1, 0, 4)
+        for u in range(2):
+            for j in (2 * u, 2 * u + 1):
+                gather_first(j, 0)
+                gather_rest(j, 1, CHUNKS, 0)
+            nc.vector.tensor_copy(
+                rest_bf0[:].rearrange("p (c i j) -> p c j i", i=2, j=PACK)[:, :, 2 * u : 2 * u + 2, :],
+                picked[0][:].rearrange("p (j c i) -> p c j i", i=2, j=PACK)[:, :, 2 * u : 2 * u + 2, :],
+            )
+        quantize_x(0, 0, 1, first_bf0)
         round_w2(0, nc.vector.tensor_copy, 0, 2)
         round_w2(0, nc.scalar.copy, 2, 4)
+        quantize_x(0, 1, CHUNKS, rest_bf0)
         quantize_w2(0, 0, 2)
+        round_w2(1, nc.vector.tensor_copy, 0, 2)
+        round_w2(1, nc.scalar.copy, 2, 4)
         gather_first(1)
         gather_rest(1, 1, CHUNKS)
-        quantize_w2(0, 2, 4)
+        quantize_w2(0, 2, 4, 4096, "w_raw1")
+        quantize_w2(1, 0, 4)
         for u in range(2):
             for c in range(CHUNKS):
                 h_pass(0, c, (2 * u, 2 * u + 1))

@@ -92,14 +92,13 @@ def tile_picked_lora_gelu_e_kernel(
             return offsets[:, c0 * LIST_COLS : c1 * LIST_COLS]
 
         picked = [sb("picked%d" % z, [P, PACK * REST], (F32, BF16)[z]) for z in range(PASSES)]
-        first_bf0 = sb("first_bf0", [P, CHUNK * PACK], BF16)
-        rest_bf0 = sb("rest_bf0", [P, REST * PACK], BF16)
+        x_bf0 = sb("x_bf0", [P, S * PACK], BF16)
         x_bf1 = [sb("x_bf1_%d" % c, [P, CHUNK * PACK], BF16) for c in range(CHUNKS)]
         x_ops = {}
 
-        def gather_first(j, z=1, c=0):
-            dst = (first_bf0, x_bf1[c])[z][:].rearrange("p (n t) -> p t n", t=PACK)[:, j, :]
-            nc.vector.tensor_copy(dst, planes[z, j].indirect(entries(c, c + 1)))
+        def gather_first(j, c=0):
+            dst = x_bf1[c][:].rearrange("p (n t) -> p t n", t=PACK)[:, j, :]
+            nc.vector.tensor_copy(dst, planes[1, j].indirect(entries(c, c + 1)))
 
         def gather_rest(j, c0, c1, z=1):
             dst = picked[z][:, j * REST + (c0 - 1) * CHUNK : j * REST + (c1 - 1) * CHUNK]
@@ -122,10 +121,10 @@ def tile_picked_lora_gelu_e_kernel(
         w_ops = {}
         w_bf = [sb("w_bf%d" % z, [P, H * PACK], BF16) for z in range(PASSES)]
 
-        def round_w2(z, engine_copy, t0, t1):
+        def round_w2(z, engine_copy, t0, t1, m0=0, m1=P):
             dst = w_bf[z][:].rearrange("p (t m j) -> p m j t", t=PACK, j=PACK)
             src = w_raw[z][:].rearrange("p (j m t) -> p m j t", j=PACK, t=PACK)
-            engine_copy(dst[:, :, :, t0:t1], src[:, :, :, t0:t1])
+            engine_copy(dst[:, m0:m1, :, t0:t1], src[:, m0:m1, :, t0:t1])
 
         def quantize_w2(z, t0, t1, align=256, tag=None):
             n = (t1 - t0) * P
@@ -149,19 +148,23 @@ def tile_picked_lora_gelu_e_kernel(
 
         gather_first(0)
         gather_rest(0, 1, CHUNKS)
-        for u in range(2):
+        for u, direct in enumerate((128, 192)):
             for j in (2 * u, 2 * u + 1):
-                gather_first(j, 0)
-                gather_rest(j, 1, CHUNKS, 0)
+                dst = x_bf0[:, : direct * PACK].rearrange("p (n t) -> p t n", t=PACK)[:, j, :]
+                nc.vector.tensor_copy(dst, planes[0, j].indirect(offsets[:, : direct // 16]))
+                dst = picked[0][:, j * REST + direct - CHUNK : (j + 1) * REST]
+                nc.scalar.activation(dst, planes[0, j].indirect(offsets[:, direct // 16 :]), COPY)
+            skip = (direct - CHUNK) // 2
             nc.vector.tensor_copy(
-                rest_bf0[:].rearrange("p (c i j) -> p c j i", i=2, j=PACK)[:, :, 2 * u : 2 * u + 2, :],
-                picked[0][:].rearrange("p (j c i) -> p c j i", i=2, j=PACK)[:, :, 2 * u : 2 * u + 2, :],
+                x_bf0[:, CHUNK * PACK :].rearrange("p (c i j) -> p c j i", i=2, j=PACK)[:, skip:, 2 * u : 2 * u + 2, :],
+                picked[0][:].rearrange("p (j c i) -> p c j i", i=2, j=PACK)[:, skip:, 2 * u : 2 * u + 2, :],
             )
-        quantize_x(0, 0, 1, first_bf0)
-        round_w2(0, nc.vector.tensor_copy, 0, 2)
+        share = 3 * P // 4
+        round_w2(0, nc.vector.tensor_copy, 0, 2, 0, share)
+        round_w2(0, nc.scalar.copy, 0, 2, share, P)
         round_w2(0, nc.scalar.copy, 2, 4)
-        quantize_x(0, 1, CHUNKS, rest_bf0)
-        quantize_w2(0, 0, 2)
+        quantize_x(0, 0, CHUNKS, x_bf0)
+        quantize_w2(0, 0, 2, 4096, "w_raw0")
         round_w2(1, nc.vector.tensor_copy, 0, 2)
         round_w2(1, nc.scalar.copy, 2, 4)
         gather_first(1)

@@ -126,11 +126,12 @@ def tile_picked_lora_gelu_e_kernel(
             src = w_raw[z][:].rearrange("p (j m t) -> p m j t", j=PACK, t=PACK)
             engine_copy(dst[:, m0:m1, :, t0:t1], src[:, m0:m1, :, t0:t1])
 
-        def quantize_w2(z, t0, t1, align=256, tag=None):
+        def quantize_w2(z, t0, t1, align=256, tag=None, scales=None):
             n = (t1 - t0) * P
             words = sb("w2_words%d_%d" % (z, t0), [P, n], U32, align, tag)
-            scales = sb("w2_bytes%d_%d" % (z, t0), [P, n], U8)
-            nc.vector.quantize_mx(words[:].bitcast(FP8X4), scales[:], w_bf[z][:, t0 * P * PACK : t1 * P * PACK])
+            if scales is None:
+                scales = sb("w2_bytes%d_%d" % (z, t0), [P, n], U8)[:]
+            nc.vector.quantize_mx(words[:].bitcast(FP8X4), scales, w_bf[z][:, t0 * P * PACK : t1 * P * PACK])
             for t in range(t0, t1):
                 cols = slice((t - t0) * P, (t - t0 + 1) * P)
                 w_ops[z, t] = dict(lhsT=words[:, cols].bitcast(FP8X4), lhsT_scale=scales[:, cols])
@@ -165,12 +166,14 @@ def tile_picked_lora_gelu_e_kernel(
         round_w2(0, nc.scalar.copy, 2, 4)
         quantize_x(0, 0, CHUNKS, x_bf0)
         quantize_w2(0, 0, 2, 4096, "w_raw0")
+        shared_planes = sb("w2_shared_planes", [P, H], U8)
+        quantize_w2(0, 2, 4, scales=shared_planes[4:P, : 2 * P])
         round_w2(1, nc.vector.tensor_copy, 0, 2)
-        round_w2(1, nc.scalar.copy, 2, 4)
+        round_w2(1, nc.vector.tensor_copy, 2, 4, 0, P - share)
+        round_w2(1, nc.scalar.copy, 2, 4, P - share, P)
         gather_first(1)
         gather_rest(1, 1, CHUNKS)
-        quantize_w2(0, 2, 4, 4096, "w_raw1")
-        quantize_w2(1, 0, 4)
+        quantize_w2(1, 0, 4, scales=shared_planes[:])
         for u in range(2):
             for c in range(CHUNKS):
                 h_pass(0, c, (2 * u, 2 * u + 1))

@@ -169,8 +169,7 @@ def tile_picked_lora_gelu_e_kernel(
         shared_planes = sb("w2_shared_planes", [P, H], U8)
         quantize_w2(0, 2, 4, scales=shared_planes[4:P, : 2 * P])
         round_w2(1, nc.vector.tensor_copy, 0, 2)
-        round_w2(1, nc.vector.tensor_copy, 2, 4, 0, P - share)
-        round_w2(1, nc.scalar.copy, 2, 4, P - share, P)
+        round_w2(1, nc.scalar.copy, 2, 4)
         gather_first(1)
         gather_rest(1, 1, CHUNKS)
         quantize_w2(1, 0, 4, scales=shared_planes[:])

from contextlib import ExitStack

import concourse.mybir as mybir

K, T, S, H, N = 1024, 1024, 512, 512, 128
FLOPS = 2 * S * (K * H + K * N + H * N)

F32 = mybir.dt.float32
BF16 = mybir.dt.bfloat16
U32 = mybir.dt.uint32
I32 = mybir.dt.int32
U16 = mybir.dt.uint16
U8 = mybir.dt.uint8
FP8X4 = mybir.dt.float8_e4m3fn_x4
GELU = mybir.ActivationFunctionType.Gelu_apprx_tanh
COPY = mybir.ActivationFunctionType.Copy

P = 128
PACK = 4
K_PASS = P * PACK
PASSES = K // K_PASS
CHUNK = 128
CHUNKS = S // CHUNK
LIST_COLS = CHUNK // 16
REST = S - CHUNK


def tile_picked_lora_gelu_e_kernel(
    tc, xT, w1_words, w1_scales, w2, w3_words, w3_scales, offs, out
):
    nc = tc.nc
    with ExitStack() as ctx:
        keep = ctx.enter_context(tc.tile_pool(name="keep", bufs=1))
        psum = ctx.enter_context(tc.psum_pool(name="psum", bufs=1))

        def sb(name, shape, dtype, align=256, tag=None):
            return keep.tile(shape, dtype, name=name, tag=tag or name, align_bytes=align)

        planes = {}

        def load_plane_pair(z, j, queue=nc.sync):
            pair = sb("pair%d_%d" % (z, j), [P, 2 * T], F32, 4096)
            rows = xT[z * K_PASS : (z + 1) * K_PASS, :].rearrange("(p u j) c -> u p (j c)", u=2, j=2)
            queue.dma_start(pair[:], rows[j // 2])
            planes[z, j] = pair[:, :T]
            planes[z, j + 1] = pair[:, T:]

        planes[1, 0] = sb("plane1_0", [P, T], F32, 4096)[:]
        nc.scalar.dma_start(planes[1, 0], xT[K_PASS:, :].rearrange("(p j) c -> j p c", j=PACK)[0])
        zeros = sb("zeros", [P, 1], F32)
        zero_bias = sb("zero_bias", [P, 1], F32)
        nc.vector.memset(zeros[:], 0.0)
        nc.scalar.activation(zero_bias[:], zeros[:], GELU)

        w1_s = sb("w1_s", [P, PASSES, N], U8)
        w3_s = sb("w3_s", [P, N], U8)
        nc.gpsimd.memset(w1_s[:].bitcast(I32), 0)
        nc.vector.memset(w3_s[:].bitcast(I32), 0)

        offsets = keep.tile([P, S // 16], U16, name="offsets")
        w_raw = {}

        def load_plane(z, j):
            planes[z, j] = sb("plane%d_%d" % (z, j), [P, T], F32, 4096)[:]
            rows = xT[z * K_PASS : (z + 1) * K_PASS, :].rearrange("(p j) c -> j p c", j=PACK)
            nc.sync.dma_start(planes[z, j], rows[j])

        def load_w2(z):
            w_raw[z] = sb("w_raw%d" % z, [P, PACK * H], F32, 4096)
            rows = w2[z * K_PASS : (z + 1) * K_PASS, :].rearrange("(p j) c -> p (j c)", j=PACK)
            nc.sync.dma_start(w_raw[z][:], rows)

        nc.sync.dma_start(offsets[:], offs)
        load_plane_pair(0, 0)
        load_plane_pair(0, 2)
        load_w2(0)
        load_w2(1)
        for j in range(1, PACK):
            load_plane(1, j)
        w1_w = sb("w1_w", [P, PASSES, N], U32)
        w3_w = sb("w3_w", [P, N], U32)
        nc.sync.dma_start(w1_w[:].bitcast(I32), w1_words.rearrange("z p c r -> p z (c r)").bitcast(I32))
        w1_rows = w1_scales.rearrange("z (q r) c -> r q z c", r=4)
        for r in range(4):
            nc.sync.dma_start(w1_s[r:P:32, :, :].bitcast(I32), w1_rows[r].bitcast(I32))
        nc.sync.dma_start(w3_w[:].bitcast(I32), w3_words[0].rearrange("p c r -> p (c r)").bitcast(I32))
        w3_rows = w3_scales[0].rearrange("(q r) c -> r q c", r=4)
        for r in range(4):
            nc.sync.dma_start(w3_s[r:P:32, :].bitcast(I32), w3_rows[r].bitcast(I32))

        def entries(c0, c1):
            return offsets[:, c0 * LIST_COLS : c1 * LIST_COLS]

        picked = [sb("picked%d" % z, [P, PACK * REST], (F32, BF16)[z]) for z in range(PASSES)]
        x_bf0 = sb("x_bf0", [P, S * PACK], BF16)
        x_bf1 = [sb("x_bf1_%d" % c, [P, CHUNK * PACK], BF16) for c in range(CHUNKS)]
        x_ops = {}

        def gather_first(j, c=0):
            dst = x_bf1[c][:].rearrange("p (n t) -> p t n", t=PACK)[:, j, :]
            nc.vector.tensor_copy(dst, planes[1, j].indirect(entries(c, c + 1)))

        def gather_rest(j, c0, c1, z=1):
            dst = picked[z][:, j * REST + (c0 - 1) * CHUNK : j * REST + (c1 - 1) * CHUNK]
            nc.scalar.activation(dst, planes[z, j].indirect(entries(c0, c1)), COPY)

        def interleave_planes(j0, j1, c):
            src = picked[1][:].rearrange("p (j n) -> p j n", j=PACK)[:, j0:j1, (c - 1) * CHUNK : c * CHUNK]
            dst = x_bf1[c][:].rearrange("p (c i j) -> p c j i", i=4, j=PACK)[:, :, j0:j1, :]
            nc.vector.tensor_copy(dst, src.rearrange("p j (c i) -> p c j i", i=4))

        def quantize_x(z, c0, c1, grouped):
            n = (c1 - c0) * CHUNK
            words = sb("x_words%d_%d" % (z, c0), [P, n], U32)
            scales = sb("x_bytes%d_%d" % (z, c0), [P, n], U8)
            nc.vector.quantize_mx(words[:].bitcast(FP8X4), scales[:], grouped[:])
            for c in range(c0, c1):
                cols = slice((c - c0) * CHUNK, (c - c0 + 1) * CHUNK)
                x_ops[z, c] = dict(rhs=words[:, cols].bitcast(FP8X4), rhs_scale=scales[:, cols])

        w_ops = {}
        w_bf = [sb("w_bf%d" % z, [P, H * PACK], BF16) for z in range(PASSES)]

        def round_w2(z, engine_copy, t0, t1, m0=0, m1=P):
            dst = w_bf[z][:].rearrange("p (t m j) -> p m j t", t=PACK, j=PACK)
            src = w_raw[z][:].rearrange("p (j m t) -> p m j t", j=PACK, t=PACK)
            engine_copy(dst[:, m0:m1, :, t0:t1], src[:, m0:m1, :, t0:t1])

        def quantize_w2(z, t0, t1, align=256, tag=None, scales=None):
            n = (t1 - t0) * P
            words = sb("w2_words%d_%d" % (z, t0), [P, n], U32, align, tag)
            if scales is None:
                scales = sb("w2_bytes%d_%d" % (z, t0), [P, n], U8)[:]
            nc.vector.quantize_mx(words[:].bitcast(FP8X4), scales, w_bf[z][:, t0 * P * PACK : t1 * P * PACK])
            for t in range(t0, t1):
                cols = slice((t - t0) * P, (t - t0 + 1) * P)
                w_ops[z, t] = dict(lhsT=words[:, cols].bitcast(FP8X4), lhsT_scale=scales[:, cols])

        first_banks = [psum.tile([P, 2, CHUNK], F32, name="first_bank%d" % u, tag="first%d" % u) for u in range(2)]
        h_banks = {c: psum.tile([P, PACK, CHUNK], F32, name="h_bank%d" % c) for c in range(1, CHUNKS)}

        def h_pass(z, c, ts):
            for t in ts:
                bank, slot, slots = (first_banks[t // 2], t % 2, 2) if c == 0 else (h_banks[c], t, PACK)
                nc.tensor.matmul_mx(
                    bank[:, slot, :],
                    start=(z == 0 and slot == 0), stop=(z == PASSES - 1 and slot == slots - 1), **w_ops[z, t], **x_ops[z, c]
                )

        gather_first(0)
        gather_rest(0, 1, CHUNKS)
        for u, direct in enumerate((128, 192)):
            for j in (2 * u, 2 * u + 1):
                dst = x_bf0[:, : direct * PACK].rearrange("p (n t) -> p t n", t=PACK)[:, j, :]
                nc.vector.tensor_copy(dst, planes[0, j].indirect(offsets[:, : direct // 16]))
                dst = picked[0][:, j * REST + direct - CHUNK : (j + 1) * REST]
                nc.scalar.activation(dst, planes[0, j].indirect(offsets[:, direct // 16 :]), COPY)
            skip = (direct - CHUNK) // 2
            nc.vector.tensor_copy(
                x_bf0[:, CHUNK * PACK :].rearrange("p (c i j) -> p c j i", i=2, j=PACK)[:, skip:, 2 * u : 2 * u + 2, :],
                picked[0][:].rearrange("p (j c i) -> p c j i", i=2, j=PACK)[:, skip:, 2 * u : 2 * u + 2, :],
            )
        share = 3 * P // 4
        round_w2(0, nc.vector.tensor_copy, 0, 2, 0, share)
        round_w2(0, nc.scalar.copy, 0, 2, share, P)
        round_w2(0, nc.scalar.copy, 2, 4)
        quantize_x(0, 0, CHUNKS, x_bf0)
        quantize_w2(0, 0, 2, 4096, "w_raw0")
        shared_planes = sb("w2_shared_planes", [P, H], U8)
        quantize_w2(0, 2, 4, scales=shared_planes[4:P, : 2 * P])
        round_w2(1, nc.vector.tensor_copy, 0, 2)
        round_w2(1, nc.scalar.copy, 2, 4)
        gather_first(1)
        gather_rest(1, 1, CHUNKS)
        quantize_w2(1, 0, 4, scales=shared_planes[:])
        for u in range(2):
            for c in range(CHUNKS):
                h_pass(0, c, (2 * u, 2 * u + 1))
        gather_first(2)
        gather_rest(2, 1, 2)
        gather_rest(2, 2, CHUNKS)
        interleave_planes(0, 3, 1)
        gather_first(3)
        gather_first(3, c=1)
        gather_rest(3, 2, CHUNKS)
        for c in range(2):
            quantize_x(1, c, c + 1, x_bf1[c])
            h_pass(1, c, range(PACK))
        for c in range(2, CHUNKS):
            interleave_planes(0, 4, c)
        for c in range(2, CHUNKS):
            quantize_x(1, c, c + 1, x_bf1[c])
            h_pass(1, c, range(PACK))

        for c in range(CHUNKS):
            h_bf = sb("h_bf%d" % c, [P, CHUNK * PACK], BF16)
            halves = ((0, CHUNK // 2), (CHUNK // 2, CHUNK)) if c == CHUNKS - 1 else ((0, CHUNK),)
            if c == 0:
                pairs = sb("h_pairs", [P, 2, 2 * CHUNK], BF16)
                for u in range(2):
                    nc.scalar.activation(
                        pairs[:, u, :].rearrange("p (n t) -> p n t", t=2), first_banks[u][:].rearrange("p t n -> p n t"), GELU
                    )
                nc.vector.tensor_copy(
                    h_bf[:].bitcast(I32).rearrange("p (n u) -> p n u", u=2), pairs[:].bitcast(I32).rearrange("p u n -> p n u")
                )
            else:
                for a, b in halves:
                    nc.scalar.activation(
                        h_bf[:, a * PACK : b * PACK].rearrange("p (n t) -> p n t", t=PACK),
                        h_banks[c][:, :, a:b].rearrange("p t n -> p n t"), GELU,
                        bias=(zero_bias[:] if c == 1 else 0.0),
                    )
            out_bank = psum.tile([P, CHUNK], F32, name="out_bank%d" % c, tag=("first0" if c == CHUNKS - 1 else "out%d" % c))
            for z in range(PASSES):
                nc.tensor.matmul_mx(
                    out_bank[:], lhsT=w1_w[:, z, :].bitcast(FP8X4), lhsT_scale=w1_s[:, z, :],
                    start=(z == 0), stop=False, **x_ops[z, c]
                )
            h_words = sb("h_words%d" % c, [P, CHUNK], U32)
            h_bytes = sb("h_bytes%d" % c, [P, CHUNK], U8)
            for a, b in halves:
                nc.vector.quantize_mx(h_words[:, a:b].bitcast(FP8X4), h_bytes[:, a:b], h_bf[:, a * PACK : b * PACK])
            nc.tensor.matmul_mx(
                out_bank[:], lhsT=w3_w[:].bitcast(FP8X4), lhsT_scale=w3_s[:],
                rhs=h_words[:].bitcast(FP8X4), rhs_scale=h_bytes[:], start=False, stop=True,
            )
            result = sb("result%d" % c, [P, CHUNK], F32)
            if c > 0:
                nc.scalar.copy(result[:], out_bank[:])
            else:
                nc.vector.tensor_copy(result[:], out_bank[:])
            nc.sync.dma_start(out[:, c * CHUNK : (c + 1) * CHUNK], result[:])
